import numpy as np, ml_dtypes
CORES = [8,136,40,168]
N = 4
BF = ml_dtypes.bfloat16
def gentries(a):
    return np.ascontiguousarray(a.reshape(8, 16, -1).transpose(0, 2, 1)).reshape(8, -1)
def gtable(e):
    e = np.asarray(e); return np.ascontiguousarray(e.reshape(8, -1, 16).transpose(0, 2, 1)).reshape(128, -1).astype(np.int32)
V, C, H, NCL, ST, Q = 1024, 64, 2048, 8, 5, 16
LANE = np.arange(16)
def look(xs, l):
    a = np.take_along_axis(xs, l[:, None, :], 2).reshape(8, 16, C, 16)
    return a, np.max(a, axis=3) - np.min(a, axis=3)
def best(s, w, tag):
    u = np.add.reduce(w[:, :, :, None] * s[:, :, None, :], axis=1) & (H - 1)
    u1, u2 = u[:, 0], u[:, 1]
    h = (((u1 * u2) >> 5)[:, None, :] + (2 * LANE[:, None] + 1) * u2[:, None, :]) & (H - 1)
    cost = np.stack([np.add.reduce(np.abs(np.take_along_axis(tag, h[:, m:m + 1], 2) - s), axis=1) for m in range(16)], axis=1)
    m = np.argmin(cost, axis=1)
    return h, np.min(cost, axis=1), np.take_along_axis(h, m[:, None, :], 1)[:, 0]
def start(x, l, w, tag):
    o = []
    for r in range(N):
        s = look(x[r], l[r, :, r % NCL])[1]; h, least, hs = best(s, w[r], tag[r]); o.append((s, h, least))
    return [np.stack(z) for z in zip(*o)]
def mid(rng, least):
    return np.take_along_axis(np.sort(least, axis=-1), rng.integers(C // 5, 4 * C // 5, (N, 8, 1)), -1)[..., 0]
def parts(rng):
    x = rng.integers(0, 256, (N, 8, 16, V)); l = np.argsort(rng.random((N, 8, NCL, V)), axis=-1)
    tag = np.minimum((256 * rng.beta(15.0, 2.0, (N, 8, 16, H))).astype(np.int64), 255)
    e = np.argsort(rng.random((N, 8, H, 16)), axis=-1); f = np.argsort(e, axis=-1)
    return x, l, tag, np.ascontiguousarray((e + 16 * f).transpose(0, 1, 3, 2)), rng.integers(1, 256, (N, 8, 16, 2))
def plant(rng, s, h, tag, ids, n, dev, used, copies=1):
    done = []
    for i in ids:
        if len(done) == n: break
        i = int(i); free = sorted(set(int(z) for z in h[:, i]) - used)
        if len(free) < copies: continue
        for j in rng.permutation(len(free))[:copies]:
            z = free[int(j)]; used.add(z); p = int(rng.integers(0, 16)); tag[:, z] = s[:, i]
            tag[p, z] = s[p, i] + (dev if s[p, i] < 128 else -dev)
        done.append(i)
    return done
def wear(rng, x, ix, s):
    lo = (rng.random(s.shape) * (256 - s)).astype(np.int64); k = rng.integers(0, 16, s.shape); k2 = (k + rng.integers(1, 16, s.shape)) & 15
    a = lo[..., None] + (rng.random(s.shape + (16,)) * (s[..., None] + 1)).astype(np.int64)
    np.put_along_axis(a, k[..., None], lo[..., None], 2); np.put_along_axis(a, k2[..., None], (lo + s)[..., None], 2)
    x[:, ix] = a.reshape(16, -1)
def still(rng, x, ix, tag):
    s = rng.integers(20, 181, (16, C)); s[:2] = 0; z = np.zeros(C, np.int64)
    o = rng.permutation(C); a = np.sort(o[:Q + 3]); b = o[Q + 3:]
    z[a] = H // 2 + 2 + 2 * rng.permutation(H // 4 - 1)[:Q + 3]; z[b] = 1 + 2 * rng.permutation(H // 2 - 1)[:C - Q - 3]
    z[b[0]] = H - 1
    z[a[Q - 1]] = z[a[0]]; z[a[Q - 3]] = z[a[1]]; z[a[Q - 2]] = z[a[1]]
    s[2] = z >> 4; s[3] = z & 15
    v = s[4:, a[0]]; s[4:, a[Q - 1]] = np.where(v < 100, v + 100, v - 100)
    s[4:, a[Q - 3]] = s[4:, a[1]] - 3; s[4:, a[Q - 2]] = s[4:, a[1]] + 3
    s[:, a[2]] = 0; s[:, b[1]] = np.where(LANE < 4, 0, 3); tag[:, 0] = np.where(LANE < 4, 0, 6)
    c = np.concatenate([b[:1], b[10:]]); tag[:, z[c]] = s[:, c]
    for j in range(8):
        i = int(b[2 + j]); s[:4, i] = np.array([255, 9, 255, 7] if j < 4 else [255, 7, 255, 9])
        u1 = (4080 + int(s[1, i])) & (H - 1); u2 = (4080 + int(s[3, i])) & (H - 1)
        tag[:, (((u1 * u2) >> 5) + (8 * (j & 3) + 1) * u2) & (H - 1)] = s[:, i]
    wear(rng, x, ix, s)
def pack(x, l, tag, ef, w, th):
    b = lambda a, n: np.ascontiguousarray(a).reshape(N, 128, n).astype(np.float32).astype(BF)
    return {"x": b(x, V), "nb": np.stack([gtable(a.reshape(8, -1)) for a in l]), "tag": b(tag, H), "ef": b(ef, H), "w": b(w, 2),
            "th": np.ascontiguousarray(np.repeat(th, 16, axis=1)[:, :, None]).astype(np.int32)}
def setup_inputs(rng):
    x, l, tag, ef, w = parts(rng); s, h, least = start(x, l, w, tag)
    return pack(x, l, tag, ef, w, mid(rng, least))
def setup_inputs_room(rng):
    x, l, tag, ef, w = parts(rng); s, h, least = start(x, l, w, tag); th = np.zeros((N, 8), np.int64)
    for r in range(N):
        for g in range(8):
            n = int(rng.choice(np.array([0, 1, Q - 1, Q, Q + 1, C]))); t = int(rng.choice(np.array([0, 1, 20])))
            if r == 0: n = (Q, Q + 1, Q - 1, 0, 1, C, Q, Q + 1)[g]
            if n == 0:
                th[r, g] = 4080; continue
            used = set(); ids = rng.permutation(C); done = set(plant(rng, s[r, g], h[r, g], tag[r, g], ids, C - n, t, used))
            plant(rng, s[r, g], h[r, g], tag[r, g], [i for i in ids if int(i) not in done], n // 2, t + 1, used); th[r, g] = t
    return pack(x, l, tag, ef, w, th)
def setup_inputs_ties(rng):
    x, l, tag, ef, w = parts(rng); s, h, least = start(x, l, w, tag); th = np.zeros((N, 8), np.int64)
    for r in range(N):
        for g in range(8):
            th[r, g] = int(rng.choice(np.array([0, 1, 20])))
            plant(rng, s[r, g], h[r, g], tag[r, g], rng.permutation(C), C // 2, int(th[r, g]), set(), 2)
    for g in (3, 5): tag[:, g] = tag[:, g, :, :1].copy()
    t = mid(rng, start(x, l, w, tag)[2])
    for g in (3, 5): th[:, g] = t[:, g]
    return pack(x, l, tag, ef, w, th)
def setup_inputs_hash(rng):
    x, l, tag, ef, w = parts(rng)
    w[:, 0, :, 1] = 0; w[:, 1, :, 0] = 0; w[:, 2] = 0; w[:, 2, 5] = np.array([3, 255]); w[:, 3] = 255; w[:, 4, :, 1] = 128
    x[:, 5] = 255 * rng.integers(0, 2, (N, 16, V)); x[:, 6] = rng.integers(0, 256, (N, 16, 1))
    tag[0, 5] = rng.integers(0, 5, (16, H)); tag[1, 5] = 0
    w[:, 7] = 0; w[:, 7, :4] = np.array([[16, 0], [1, 0], [0, 16], [0, 1]]); l[:, 7] = l[:, 7, :1].copy()
    for r in range(N): still(rng, x[r, 7], l[r, 7, 0], tag[r, 7])
    th = mid(rng, start(x, l, w, tag)[2]); th[::2, 5] = np.maximum(th[::2, 5] - 1, 0); th[1::2, 0] = 4080; th[:, 7] = 40
    return pack(x, l, tag, ef, w, th)
def setup_inputs_ends(rng):
    x, l, tag, ef, w = parts(rng)
    l[:, 0] = np.arange(V); l[:, 1] = np.arange(V)[::-1]; l[:, 2] = l[:, 2, :1].copy()
    ef[:, 4] = (17 * LANE)[:, None]; ef[:, 5] = (17 * (15 - LANE))[:, None]; ef[:, 6] = (((LANE + 1) & 15) + 16 * ((LANE + 15) & 15))[:, None]
    q = rng.permutation(N); x[q[2:4]] = rng.integers(0, 8, (2, 8, 16, V)); tag[q[2:4]] = rng.integers(240, 256, (2, 8, 16, H))
    th = mid(rng, start(x, l, w, tag)[2]); th[q[0]] = 0; th[q[1]] = 4080
    return pack(x, l, tag, ef, w, th)
def setup_inputs_spread(rng):
    x, l, tag, ef, w = parts(rng)
    x = (np.exp2(8 * rng.random((N, 8, 1, V))) * rng.random((N, 8, 16, V))).astype(np.int64)
    tag = (np.exp2(8 * rng.random((N, 8, 1, H))) * rng.random((N, 8, 16, H))).astype(np.int64)
    x = np.minimum(x, 255); tag = np.minimum(tag, 255)
    w = np.minimum(np.exp2(8 * rng.random((N, 8, 16, 2))).astype(np.int64), 255)
    return pack(x, l, tag, ef, w, mid(rng, start(x, l, w, tag)[2]))
def check_inputs(d):
    bad = []
    for k, hi in (("x", 255), ("nb", V - 1), ("tag", 255), ("ef", 255), ("w", 255), ("th", 4080)):
        v = np.asarray(d[k]).astype(np.float32)
        if not (np.all(v >= 0) and np.all(v <= hi) and np.all(v == np.floor(v))): bad.append("range of " + k)
    if bad: return bad
    l = np.stack([gentries(a) for a in d["nb"]]).reshape(N, 8, NCL, V)
    if np.any(np.sort(l, axis=-1) != np.arange(V)): bad.append("sites of a class all different")
    b = np.asarray(d["ef"]).astype(np.float32).astype(np.int64).reshape(N, 8, 16, H); e = b & 15; f = b >> 4
    if np.any(np.sort(e, axis=2) != LANE[:, None]) or np.any(np.take_along_axis(f, e, 2) != LANE[:, None]): bad.append("e a permutation, f its inverse")
    t = np.asarray(d["th"]).reshape(N, 8, 16)
    if np.any(t != t[:, :, :1]): bad.append("th alike in a group")
    return bad
def reference(x, nb, tag, ef, w, th):
    whole = lambda a, n: a.astype(np.float32).astype(np.int64).reshape(N, 8, 16, n)
    xs, tg, pf, ws = whole(x, V), whole(tag, H), whole(ef, H), whole(w, 2)
    lim = th.astype(np.int64).reshape(N, 8, 16)[:, :, :1]
    l = np.stack([gentries(a) for a in nb]).astype(np.int64).reshape(N, 8, NCL, V)
    cl = [r % NCL for r in range(N)]
    for t in range(ST):
        sig, home, miss = [], [], []
        for r in range(N):
            ix = l[r, :, cl[r]]; a, s = look(xs[r], ix)
            h, least, hs = best(s, ws[r], tg[r]); hit = least <= lim[r]
            f = np.take_along_axis(pf[r] >> 4, hs[:, None, :], 2)
            f = np.where(hit[:, None, :], f, LANE[:, None])
            a = np.take_along_axis(a, f.transpose(0, 2, 1)[:, None, :, :], 3).reshape(8, 16, V)
            for g in range(8): xs[r, g][:, ix[g]] = a[g]
            sig.append(s); home.append(h[:, 0]); miss.append(~hit); cl[r] = int(np.sum(least)) & (NCL - 1)
        new = []
        for r in range(N):
            q = (r + 1 + t % (N - 1)) % N
            far = best(sig[r], ws[q], tg[q])[2]; back = np.take_along_axis(pf[q], far[:, None, :], 2)
            for g in range(8):
                i = np.flatnonzero(miss[r][g])[:Q]
                col, first = np.unique(home[r][g, i], return_index=True); i = i[first]
                new.append((r, g, col, sig[r][g][:, i], back[g][:, i]))
        for r, g, col, s, b in new:
            tg[r, g][:, col] = s; pf[r, g][:, col] = (b >> 4) + 16 * (b & 15)
    return {"y": xs.reshape(N, 128, V).astype(np.float32).astype(BF)}

@@ -1,0 +1,679 @@
+from concourse.mybir import AluOpType, AxisListType, ActivationFunctionType
+
+AL = AluOpType
+AF = ActivationFunctionType
+SCRATCH = {
+    "ab": ("sbuf", [128, 23552], "bfloat16"),
+    "af": ("sbuf", [128, 6400], "float32"),
+    "ai": ("sbuf", [128, 4608], "int32"),
+    "au": ("sbuf", [128, 2304], "uint16"),
+    "pu": ("psum", [128, 512], "float32"),
+    "pk": ("psum", [128, 512], "float32"),
+    "pp": ("psum", [128, 512], "float32"),
+    "pc": ("psum", [128, 512], "float32"),
+    "pr": ("psum", [128, 512], "float32"),
+    "pq": ("psum", [128, 512], "float32"),
+}
+STEPS, V, H = 5, 1024, 2048
+SEMAPHORES = (["cv", "cs", "cp", "cg", "sent", "sig"] + ["d%d" % k for k in range(16)]
+              + ["req%d" % t for t in range(STEPS - 1)] + ["rep%d" % t for t in range(STEPS - 1)])
+PSUM = ("pu", "pk", "pp", "pc", "pr", "pq")
+SIZE = {"ab": 2, "af": 4, "ai": 4, "au": 2}
+
+CFG = {"xv": 20, "pv": 28, "iv": 28, "x0": 32, "lastv": 32, "chunks": ((5, "s"), (5, "s"), (4, "s"), (2, "s")),
+       "parts": (16, 16, 16, 16), "on_s": ("b1", "b2", "se2", "sj", "un"), "early": 1, "first": 2500,
+       "iters": 400, "swaps": 10000, "heat": 300.0, "seed": 1}
+MODELS = ((1.0, 1.4, 3.4, 0.75, 80.0, 2200.0, 2300.0), (0.85, 1.0, 1.6, 0.5, 40.0, 1800.0, 1600.0),
+          (1.2, 2.1, 6.0, 1.0, 150.0, 2600.0, 3500.0))
+ORDER = {}
+
+
+def nel(r):
+    return len(range(r[1], r[2], r[3]))
+
+
+def sl(r, a, b, s=1):
+    return (r[0], r[1] + a, r[1] + b, s)
+
+
+def build(T, rank, core, topo, cfg):
+    ops = []
+    top = {"ab": 0, "af": 0, "ai": 0, "au": 0}
+    ons = cfg["on_s"]
+    site = [0]
+
+    def new(a, n):
+        q = 32 // SIZE[a]
+        s = top[a]
+        top[a] = s + (n + q - 1) // q * q
+        assert top[a] <= SCRATCH[a][1][1], a
+        return (a, s, s + n, 1)
+
+    def ap(r):
+        if r[0] == "ind":
+            return ap(r[1]).indirect(ap(r[2]))
+        if r[3] == 1:
+            return T[r[0]][:, r[1]:r[2]]
+        return T[r[0]][:, r[1]:r[2]:r[3]]
+
+    def val(x):
+        return ap(x) if isinstance(x, tuple) else x
+
+    def add(eng, fn, ins, out, cost, kind="c", lat=(0, 0, 0), after=(), sem=None):
+        rd, wr = [], []
+        for x in ins:
+            if isinstance(x, tuple):
+                rd += [x[1], x[2]] if x[0] == "ind" else [x]
+        if out is not None:
+            if out[0] == "ind":
+                wr, rd = [out[1]], rd + [out[2]]
+            else:
+                wr = [out]
+        site[0] += 1
+        ops.append({"site": site[0], "e": eng, "fn": fn, "r": rd, "w": wr, "c": cost, "k": kind, "lat": lat,
+                    "after": list(after), "sem": sem})
+        return len(ops) - 1
+
+    def ind(win, off):
+        return ("ind", win, off)
+
+    def two(xs):
+        return all(x[0] in ("ab", "au") for x in xs)
+
+    def size(out, ins, f, fix=0):
+        if out[0] == "ind":
+            return (50 + fix, 0, 0, 16 * nel(out[2]), 0)
+        if ins and ins[0][0] == "ind":
+            return (50 + fix, 0, 16 * nel(ins[0][2]), 0, 0)
+        return (fix, max(64, f * nel(ins[0] if ins else out)), 0, 0, 0)
+
+    def cp(out, a):
+        return add("v", lambda q: q.tensor_copy(ap(out), ap(a)), [a], out, size(out, [a], 0.5 if two([out, a]) else 1))
+
+    def ts(out, a, s1, o0, s2=None, o1=None):
+        if o1 is None:
+            fn = lambda q: q.tensor_scalar(ap(out), ap(a), val(s1), None, o0)
+        else:
+            fn = lambda q: q.tensor_scalar(ap(out), ap(a), val(s1), val(s2), o0, o1)
+        return add("v", fn, [a, s1, s2], out, size(out, [a], 0.5 if two([out, a]) else 1))
+
+    def tt(out, a, b, o):
+        f = 1 if a[0] in PSUM or b[0] in PSUM else 2
+        return add("v", lambda q: q.tensor_tensor(ap(out), ap(a), ap(b), o), [a, b], out, size(out, [a], f))
+
+    def scan(out, a, b, o0, o1):
+        f = 0.5 if two([out, a, b]) else 1
+        return add("v", lambda q: q.tensor_tensor_scan(ap(out), ap(a), ap(b), 0.0, o0, o1), [a, b], out, size(out, [a], f))
+
+    def red(out, a, o, absv=False):
+        return add("v", lambda q: q.tensor_reduce(ap(out), ap(a), AxisListType.X, o, apply_absolute_value=absv),
+                   [a], out, size(out, [a], 1))
+
+    def ms(out, c):
+        return add("v", lambda q: q.memset(ap(out), c), [], out, size(out, [], 0.5 if two([out]) else 1))
+
+    def act(out, a, func=AF.Identity, bias=None, scale=None):
+        kw = {}
+        if bias is not None:
+            kw["bias"] = bias
+        if scale is not None:
+            kw["scale"] = scale
+        return add("s", lambda q: q.activation(ap(out), ap(a), func, **{k: val(x) for k, x in kw.items()}),
+                   [a, bias, scale], out, size(out, [a], 1, 15))
+
+    def aff(name, out, a, scale, bias):
+        if name in ons:
+            return act(out, a, AF.Identity, bias, scale)
+        if bias is None:
+            return ts(out, a, scale, AL.mult)
+        return ts(out, a, scale, AL.mult, bias, AL.add)
+
+    def move(name, out, a):
+        return act(out, a, AF.Copy) if name in ons else cp(out, a)
+
+    def mm(out, l, r, start, stop):
+        return add("p", lambda q: q.matmul(ap(out), ap(l), ap(r), start, stop), [l, r], out, (0, 0, 0, 0, max(64, nel(r))))
+
+    def iota(out, pat, base, cm=0):
+        if out[0] == "ai":
+            fn = lambda q: q.iota(ap(out), pat, base, cm)
+        else:
+            fn = lambda q: q.iota(ap(out), pat, base, cm, allow_small_or_imprecise_dtypes=True)
+        return add("g", fn, [], out, (130, 2 * nel(out), 0, 0, 0))
+
+    nd, nr = [0], []
+
+    def dma(eng, fo, fi, ins, out, nbytes, after=()):
+        s = "d%d" % nd[0]
+        nd[0] += 1
+        return add(eng, lambda q: q.dma_start(fo(), fi()), ins, out, (60, 0, 0, 0, 0), "d", (nbytes / 200.0, 1, 0), after, s)
+
+    def send(src, land, dst_rank, sem):
+        dst = T.cores[dst_rank]
+        rid, pid = topo.addr(dst, core)
+        m = topo.mask(core, dst)
+        n = len(topo.engines(core, dst))
+        k = add("g", lambda q: q.remote_dma(ap(land), ap(src), T.sem[sem], T.sem.sent, pid, rid, m), [src], None,
+                (300 + (0 if nr else cfg["first"]), 0, 0, 0, 0), "r", sem=n)
+        nr.append(k)
+        return add("x", None, [], land, (0, 0, 0, 0, 0), "x", (0, 0, 1), [k], (sem, n))
+
+    def wide(out, win, lst, nv):
+        cp(sl(out, 0, 16 * nv), ind(win, sl(lst, 0, nv)))
+        act(sl(out, 16 * nv, V), ind(win, sl(lst, nv, 64)), AF.Copy)
+
+    B_, F_, I_, U_ = "ab", "af", "ai", "au"
+    N = len(T.cores)
+    X0, tag, ef = new(B_, V), new(B_, H + 32), new(B_, H + 32)
+    nb0, nb, wb, thi = new(I_, 64), new(I_, 512), new(B_, 2), new(I_, 1)
+    c0 = rank % 8
+    k0 = dma("y", lambda: ap(nb0), lambda: T.nb[:, 64 * c0:64 * c0 + 64], [], nb0, 32768)
+    kx = dma("s", lambda: ap(X0), lambda: T.x[:], [], X0, 262144)
+    dma("s", lambda: ap(wb), lambda: T.w[:], [], wb, 262144)
+    dma("y", lambda: ap(sl(tag, 0, H)), lambda: T.tag[:], [], sl(tag, 0, H), 786432)
+    dma("y", lambda: ap(sl(ef, 0, H)), lambda: T.ef[:], [], sl(ef, 0, H), 786432, [k0])
+    dma("y", lambda: ap(thi), lambda: T.th[:], [], thi, 786432, [k0])
+    dma("y", lambda: ap(nb), lambda: T.nb[:], [], nb, 786432, [kx])
+
+    def col():
+        return new(F_, 1)
+    pI, t1, t2 = new(I_, 1), new(I_, 1), new(I_, 1)
+    iota(pI, [[0, 1]], 0, 1)
+    io = new(B_, 144)
+    iota(io, [[1, 144]], 0)
+    Kw = new(B_, 64)
+    iota(Kw, [[0, 4], [1, 16]], 0)
+    j8 = new(F_, 8)
+    iota(j8, [[64, 2], [1, 4]], 0)
+    bI = new(B_, 64)
+    iota(bI, [[1, 4], [0, 16]], 0)
+    vals = new(F_, V)
+    iota(sl(vals, 0, 512), [[16, 8], [256, 4], [1, 16]], 32)
+    iota(sl(vals, 512, V), [[16, 8], [256, 4], [1, 16]], 160)
+    cP = new(F_, 64)
+    iota(cP, [[256, 4], [1024, 16]], 0)
+    CWall = new(B_, 192 * STEPS)
+    for t in range(STEPS - 1 + cfg["early"]):
+        iota(sl(CWall, 192 * t, 192 * t + 192), [[0, 192]], 0)
+    if "se2" in ons:
+        rep16 = new(U_, 16)
+        cp(rep16, sl(io, 0, 16))
+    else:
+        Z2 = new(B_, 256)
+        iota(Z2, [[0, 256]], 0)
+    lane, pF, l4, colb, lane4, c15, cb, c4, cl, hl_ = [col() for _ in range(10)]
+    ts(t1, pI, 15, AL.bitwise_and)
+    cp(lane, t1)
+    ts(t2, pI, 3, AL.bitwise_and)
+    cp(l4, t2)
+    cp(pF, pI)
+    ts(colb, l4, 15.75, AL.mult)
+    ts(colb, lane, 0.25, AL.mult, colb, AL.add)
+    baseQ, list0 = new(F_, 4), new(U_, 4)
+    ts(baseQ, sl(io, 0, 4), 4.0, AL.mult, colb, AL.add)
+    cp(list0, baseQ)
+    KW = 16 * max(32, cfg["xv"], 64 - cfg["xv"], cfg["x0"], 64 - cfg["x0"])
+    keep, reset, Z, rb = new(B_, KW), new(B_, KW), new(B_, V), new(B_, 64)
+    ms(keep, 1.0)
+    ms(sl(keep, 0, KW, 16), 0.0)
+    ts(reset, keep, -256.0, AL.mult, 256.0, AL.add)
+    ms(Z, 0.0)
+    act(rb, sl(reset, 0, 64), scale=512.0)
+    ts(c15, lane, -1.0, AL.mult, pF, AL.add)
+    ts(c15, c15, 15.0, AL.add)
+    act(cb, c15, scale=-1.0, bias=7.5)
+    act(c4, c15, scale=-1.0, bias=1.5)
+    act(hl_, lane, scale=-0.5, bias=7.5)
+    act(cl, c15, scale=-1.0, bias=hl_)
+    act(lane4, lane, scale=4.0)
+    io128 = sl(io, 0, 128)
+    aB, aL, a4, negB, Id, nL = new(B_, 128), new(B_, 128), new(B_, 144), new(B_, 128), new(B_, 128), new(B_, 128)
+    act(aB, io128, AF.Abs, bias=cb)
+    ts(negB, aB, 8.0, AL.is_lt, -1.0, AL.mult)
+    act(aL, io128, AF.Abs, bias=cl)
+    ts(nL, aL, hl_, AL.is_le, -1.0, AL.mult)
+    W1, W2 = new(B_, 128), new(B_, 128)
+    ts(W1, aB, 8.0, AL.is_lt, sl(wb, 0, 1), AL.mult)
+    ts(W2, aB, 8.0, AL.is_lt, sl(wb, 1, 2), AL.mult)
+    who = [w for (_, w) in cfg["chunks"]]
+    Wd, W4 = {}, {}
+    for f in ([-16, 32] if "v" in who else []) + ([16] if "s" in who else []):
+        Wd[f] = new(B_, 144)
+        ts(Wd[f], io, c15, AL.is_equal, float(f), AL.mult)
+    act(a4, io, AF.Abs, bias=c4)
+    for f in ([16] if "r2" in ons else [-16, 32]):
+        W4[f] = new(B_, 144)
+        ts(W4[f], a4, 2.0, AL.is_lt, float(f), AL.mult)
+    ts(Id, io128, pF, AL.is_equal)
+    Dr = []
+    for r in range(4):
+        cr, d = col(), new(B_, 128)
+        act(cr, lane, bias=65.0 + 16 * r)
+        act(d, Id, scale=cr)
+        Dr.append(d)
+    ones = new(B_, 128)
+    silu = act(ones, sl(keep, 0, 128), AF.Silu, scale=0.0, bias=64.0)
+    ops[silu]["c"] = (1300, 128, 0, 0, 0)
+    K2a, K2 = new(B_, 64), new(B_, 64)
+    ts(K2a, bI, l4, AL.not_equal, 65536.0, AL.mult)
+    tt(K2, K2a, Kw, AL.max)
+    cPos = new(B_, 5)
+    act(sl(cPos, 0, 4), sl(io, 0, 4), scale=16.0, bias=lane)
+    act(sl(cPos, 4, 5), lane, scale=-1.0, bias=64.0)
+    J8, JZ = new(U_, 8), new(U_, 4)
+    ts(J8, j8, lane4, AL.add)
+    ts(JZ, sl(j8, 0, 4), lane4, AL.add, 16.0, AL.mult)
+    mJ = new(B_, 128)
+    ts(sl(mJ, 0, 64), Kw, lane, AL.is_equal)
+    act(sl(mJ, 64, 128), sl(mJ, 0, 64), scale=2.0)
+    upper, cadd = new(B_, 16), new(F_, 32)
+    ts(upper, sl(Kw, 0, 16), lane, AL.is_ge, 4096.0, AL.mult)
+    c1, qc, dum, thr, nthr, lane17 = [col() for _ in range(6)]
+    act(c1, lane, scale=64.0, bias=32.0)
+    act(sl(cadd, 0, 16), sl(io, 0, 16), scale=0.0, bias=32.0)
+    act(sl(cadd, 16, 32), sl(io, 0, 16), scale=0.0, bias=c1)
+    act(qc, lane, scale=-1.0, bias=1024.0)
+    act(dum, lane, bias=float(H + 1))
+    ts(thr, thi, 16.0, AL.mult, 15.0, AL.add)
+    act(nthr, thr, scale=-float(H))
+    act(lane17, lane, scale=17.0)
+    act(sl(ef, H, H + 32), sl(io, 0, 32), scale=0.0, bias=lane17)
+    act(sl(tag, H, H + 32), sl(io, 0, 32), scale=0.0)
+
+    A, MX, MN, SE, D, R, A2, X1 = [new(B_, V) for _ in range(8)]
+    SE2, D2, R2 = new(B_, 256), new(B_, 256), new(B_, 256)
+    W = new(F_, V)
+    tagw, efw = sl(tag, 0, H), sl(ef, 0, H + 32)
+    P = lambda n, a, b, s=1: (n, a, b, s)
+    X = X0
+    lst, win = list0, nb0
+    for t in range(STEPS):
+        last = t == STEPS - 1
+        site[0] = 1000
+        nbl = new(U_, 64)
+        cp(nbl, ind(win, lst))
+        xv = cfg["xv"] if t else cfg["x0"]
+        wide(A, X, nbl, xv)
+        w1, w2, nbt = new(I_, 64), new(I_, 64), new(U_, 64)
+        ts(w1, nbl, 1025.0, AL.mult)
+        ts(w2, w1, 4, AL.logical_shift_right, 1023, AL.bitwise_and)
+        cp(nbt, w2)
+        a = 0
+        for n in cfg["parts"]:
+            ops[act(ind(W, sl(nbt, a, a + n)), sl(vals, 16 * a, 16 * (a + n)), AF.Silu)]["after"].append(silu)
+            a += n
+        invf, invl = new(F_, 64), new(U_, 64)
+        dma("y", lambda o=invf: ap(o), lambda: T[W[0]][0:128:16, W[1]:W[2]], [W], invf, 32768)
+        ts(invl, invf, -31.75, AL.add)
+        for a, b in ((0, 16 * xv), (16 * xv, V)):
+            scan(sl(MX, a, b), sl(keep, 0, b - a), sl(A, a, b), AL.mult, AL.max)
+            scan(sl(MN, a, b), sl(reset, 0, b - a), sl(A, a, b), AL.add, AL.min)
+        s = sl(Z, 0, V, 16)
+        tt(s, sl(MX, 15, V, 16), sl(MN, 15, V, 16), AL.subtract)
+        mm(P("pu", 0, 64), W1, s, True, True)
+        mm(P("pu", 64, 128), W2, s, True, True)
+        for a in (0, 512):
+            scan(sl(SE, a, a + 512), sl(keep, 0, 512), sl(Z, a, a + 512), AL.mult, AL.add)
+        ui, um, u1p, pm, hl = new(I_, 128), new(I_, 128), new(F_, 64), new(I_, 64), new(U_, 64)
+        cp(ui, P("pu", 0, 128))
+        ts(um, ui, H - 1, AL.bitwise_and)
+        ts(u1p, sl(um, 0, 64), c1, AL.add)
+        tt(pm, u1p, sl(um, 64, 128), AL.mult)
+        ts(sl(um, 0, 64), pm, 5, AL.logical_shift_right, H - 1, AL.bitwise_and)
+        cp(hl, sl(um, 0, 64))
+        key = P("pk", 0, 64)
+        mm(key, Id, Kw, True, False)
+        q0 = 0
+        for n, w in cfg["chunks"]:
+            a, b = 64 * q0, 64 * (q0 + n)
+            tt(sl(D, a, b), ind(tagw, sl(hl, 4 * q0, 4 * (q0 + n))), sl(SE, a, b), AL.subtract)
+            if w == "v":
+                ts(sl(R, a, b), sl(D, a, b), 0.0, AL.max)
+                for q in range(q0, q0 + n):
+                    mm(key, sl(Wd[-16], 15 - q, 143 - q), sl(D, 64 * q, 64 * q + 64), False, False)
+            else:
+                act(sl(R, a, b), sl(D, a, b), AF.Abs)
+            for q in range(q0, q0 + n):
+                mm(key, sl(Wd[32 if w == "v" else 16], 15 - q, 143 - q), sl(R, 64 * q, 64 * q + 64), False, q == 15)
+            q0 += n
+        dg, sc, b1, bq = new(F_, 128), new(F_, 128), new(F_, 4), new(F_, 4)
+        tt(dg, ind(um, J8), mJ, AL.mult)
+        scan(sc, sl(keep, 0, 128), dg, AL.mult, AL.add)
+        hq, u2q = sl(sc, 15, 64, 16), sl(sc, 79, 128, 16)
+        aff("b1", b1, u2q, qc, None)
+        tt(bq, b1, hq, AL.add)
+        pmn = new(F_, 64)
+        scan(pmn, rb, key, AL.add, AL.min)
+        mk = sl(pmn, 15, 64, 16)
+        ki, mi, tv, vi, wi, un, hb, hbl = [new(I_, 4) for _ in range(5)] + [new(F_, 4), new(F_, 4), new(U_, 4)]
+        if not last:
+            M = new(B_, 4)
+            ts(M, mk, thr, AL.is_le)
+        cp(ki, mk)
+        ts(mi, ki, 15, AL.bitwise_and)
+        tt(tv, mi, u2q, AL.mult)
+        tt(vi, tv, bq, AL.add)
+        ts(wi, vi, H - 1, AL.bitwise_and)
+        aff("un", un, mk, float(H), nthr)
+        tt(hb, wi, un, AL.max)
+        ts(hbl, hb, float(H), AL.min)
+        pf, pl = new(F_, 64), new(U_, 64)
+        tt(pf, ind(efw, hbl), cP, AL.add)
+        ts(pl, pf, 0.0625, AL.mult, -0.46875, AL.add)
+        wide(A2, A, pl, cfg["lastv"] if last else cfg["pv"])
+        X = X1
+        iv = cfg["lastv"] if last else cfg["iv"]
+        wide(X, A2, invl, iv)
+        if last:
+            dma("y", lambda: T.y[:, 0:16 * iv], lambda: ap(sl(X1, 0, 16 * iv)), [sl(X1, 0, 16 * iv)], None, 131072)
+            dma("s", lambda: T.y[:, 16 * iv:V], lambda: ap(sl(X1, 16 * iv, V)), [sl(X1, 16 * iv, V)], None, 131072)
+            break
+        site[0] = 2000
+        lm, lb, li, la, lst = new(I_, 4), new(B_, 4), new(I_, 4), new(I_, 4), new(U_, 4)
+        ts(lm, ki, 4, AL.logical_shift_right, 7, AL.bitwise_and)
+        cp(lb, lm)
+        for r in range(4):
+            mm(P("pc", 0, 1), ones, sl(lb, r, r + 1), r == 0, r == 3)
+        ts(li, baseQ, P("pc", 0, 1), AL.add)
+        ts(la, li, 511, AL.bitwise_and)
+        cp(lst, la)
+        win = nb
+        sJ = new(B_, 64)
+        move("sj", sJ, ind(Z, JZ))
+        mm(P("pp", 0, 5), Id, cPos, True, False)
+        mm(P("pp", 0, 4), nL, M, False, False)
+        for d in (1, 2, 3):
+            mm(P("pp", d, 4), negB, sl(M, 0, 4 - d), False, False)
+        for r in range(4):
+            mm(P("pp", r, r + 1), Dr[r], sl(M, r, r + 1), False, False)
+        for r in range(4):
+            mm(P("pp", 4, 5), negB, sl(M, r, r + 1), False, r == 3)
+        posl = new(U_, 4)
+        cp(posl, P("pp", 0, 4))
+        CW = sl(CWall, 192 * t, 192 * t + 192)
+        cp(ind(CW, posl), sJ)
+        sL = sl(CW, 0, 16)
+        sR, rsrc, rland = new(B_, 16), new(B_, 16), new(B_, 16)
+        hop = 1 + t % (N - 1)
+        if t < cfg["early"]:
+            sJR, posR, CR = new(B_, 64), new(U_, 4), sl(CWall, 192 * (STEPS - 1), 192 * STEPS)
+            send(sJ, sJR, (rank + hop) % N, "sig")
+            send(posl, posR, (rank + hop) % N, "req%d" % t)
+            cp(ind(CR, posR), sJR)
+            sR = sl(CR, 0, 16)
+        else:
+            send(sL, sR, (rank + hop) % N, "req%d" % t)
+        site[0] = 3000
+        mm(P("pr", 0, 16), W1, sL, True, True)
+        mm(P("pr", 32, 48), W2, sL, True, True)
+        mm(P("pr", 16, 32), W1, sR, True, True)
+        mm(P("pr", 48, 64), W2, sR, True, True)
+        if "se2" in ons:
+            act(SE2, ind(sR, rep16), AF.Copy)
+        else:
+            move("z2", sl(Z2, 0, 256, 16), sR)
+            scan(SE2, sl(keep, 0, 256), Z2, AL.mult, AL.add)
+        vi2, um2, up2, pm2, hl2 = new(I_, 64), new(I_, 64), new(F_, 32), new(I_, 32), new(U_, 16)
+        cp(vi2, P("pr", 0, 64))
+        ts(um2, vi2, H - 1, AL.bitwise_and)
+        tt(up2, sl(um2, 0, 32), cadd, AL.add)
+        tt(pm2, up2, sl(um2, 32, 64), AL.mult)
+        ts(sl(um2, 16, 48), pm2, 5, AL.logical_shift_right, H - 1, AL.bitwise_and)
+        cp(hl2, sl(um2, 32, 48))
+        tt(D2, ind(tagw, hl2), SE2, AL.subtract)
+        key2 = P("pq", 0, 64)
+        mm(key2, Id, K2, True, False)
+        if "r2" in ons:
+            act(R2, D2, AF.Abs)
+        else:
+            ts(R2, D2, 0.0, AL.max)
+            for a in range(4):
+                mm(key2, sl(W4[-16], 12 - 4 * a, 140 - 4 * a), sl(D2, 64 * a, 64 * a + 64), False, False)
+        for a in range(4):
+            mm(key2, sl(W4[16 if "r2" in ons else 32], 12 - 4 * a, 140 - 4 * a), sl(R2, 64 * a, 64 * a + 64), False, a == 3)
+        dg2, sc2, b2, k2 = new(F_, 48), new(F_, 48), col(), col()
+        tt(dg2, sl(um2, 16, 64), sl(mJ, 32, 80), AL.mult)
+        scan(sc2, sl(keep, 0, 48), dg2, AL.mult, AL.add)
+        h0c, hq2, u2q2 = sl(sc2, 15, 16), sl(sc2, 31, 32), sl(sc2, 47, 48)
+        aff("b2", b2, u2q2, qc, hq2)
+        bm, dd, mn, fl, wl = new(F_, 16), new(F_, 16), col(), col(), new(U_, 1)
+        tt(bm, sl(um2, 16, 32), upper, AL.add)
+        aff("dd", dd, bm, -1.0, h0c)
+        red(mn, dd, AL.min, True)
+        ts(fl, mn, P("pp", 4, 5), AL.min, 0.0, AL.is_le)
+        ts(wl, fl, dum, AL.mult, h0c, AL.max)
+        cp(ind(tag, wl), sL)
+        red(k2, key2, AL.min)
+        ki2, m2, v2, x2, hb2 = new(I_, 1), new(I_, 1), new(I_, 1), new(I_, 1), new(U_, 1)
+        cp(ki2, k2)
+        ts(m2, ki2, 15, AL.bitwise_and)
+        ts(v2, m2, u2q2, AL.mult, b2, AL.add)
+        ts(x2, v2, H - 1, AL.bitwise_and)
+        cp(hb2, x2)
+        e1, e2 = new(I_, 16), new(I_, 16)
+        ts(e1, ind(efw, hb2), 257.0, AL.mult)
+        ts(e2, e1, 4, AL.logical_shift_right, 255, AL.bitwise_and)
+        cp(rsrc, e2)
+        send(rsrc, rland, (rank - hop) % N, "rep%d" % t)
+        cp(ind(ef, wl), rland)
+    return ops
+
+
+def depend(ops):
+    hist = {}
+    for k, o in enumerate(ops):
+        dep = set(o["after"])
+        for isw, rs in ((False, o["r"]), (True, o["w"])):
+            for r in rs:
+                for (j, w, a, b) in hist.get(r[0], []):
+                    if r[0] in PSUM:
+                        if ops[j]["e"] != o["e"] or w or isw:
+                            dep.add(j)
+                    elif (w or isw) and a < r[2] and r[1] < b:
+                        dep.add(j)
+        for isw, rs in ((False, o["r"]), (True, o["w"])):
+            for r in rs:
+                h = hist.setdefault(r[0], [])
+                if isw:
+                    h[:] = [z for z in h if not (r[3] == 1 and r[1] <= z[2] and z[3] <= r[2])]
+                h.append((k, isw, r[1], r[2]))
+        dep.discard(k)
+        o["dep"] = sorted(dep)
+        o["hop"] = [0 if (ops[j]["e"] == "p" and o["e"] == "p") or o["e"] == "x" else 1 for j in o["dep"]]
+
+
+def times(ops, m):
+    c = [o["c"][0] + sum(o["c"][i + 1] * m[i] for i in range(4)) for o in ops]
+    return c, [o["lat"][0] + o["lat"][1] * m[5] + o["lat"][2] * m[6] for o in ops]
+
+
+def replay(ops, order, c, lat, hop):
+    fin, free = [0.0] * len(ops), {}
+    for k in order:
+        o = ops[k]
+        st = free.get(o["e"], 0.0)
+        for j, h in zip(o["dep"], o["hop"]):
+            if fin[j] + h * hop > st:
+                st = fin[j] + h * hop
+        if o["e"] != "x":
+            free[o["e"]] = st + c[k]
+        fin[k] = st + c[k] + lat[k]
+    return fin
+
+
+def schedule(ops, c, lat, hop, bias):
+    n = len(ops)
+    succ = [[] for _ in range(n)]
+    for k, o in enumerate(ops):
+        for j, h in zip(o["dep"], o["hop"]):
+            succ[j].append((k, h * hop))
+    prio = [0.0] * n
+    for k in range(n - 1, -1, -1):
+        prio[k] = c[k] + lat[k] + max([g + prio[s] for s, g in succ[k]] + [0.0])
+    prio = [p + b for p, b in zip(prio, bias)]
+    left = [len(o["dep"]) for o in ops]
+    rdy = [0.0] * n
+    free = {e: 0.0 for e in "vspgyx"}
+    cand = {e: [k for k in range(n) if left[k] == 0 and ops[k]["e"] == e] for e in free}
+    order = []
+    while len(order) < n:
+        t0, e = min((max(free[e], min(rdy[k] for k in l)), e) for e, l in cand.items() if l)
+        mine = cand[e]
+        j = max((prio[k], -k) for k in mine if rdy[k] <= t0)
+        j = -j[1]
+        best = None
+        for h in mine:
+            if prio[h] > prio[j] and rdy[h] < t0 + c[j] and (best is None or prio[h] > prio[best]):
+                if max(rdy[h] + prio[h], rdy[h] + c[h] + prio[j]) < max(t0 + prio[j], t0 + c[j] + prio[h]):
+                    best = h
+        if best is not None:
+            j = best
+        st = max(rdy[j], free[e])
+        if e != "x":
+            free[e] = st + c[j]
+        fin = st + c[j] + lat[j]
+        mine.remove(j)
+        order.append(j)
+        for s, g in succ[j]:
+            rdy[s] = max(rdy[s], fin + g)
+            left[s] -= 1
+            if left[s] == 0:
+                cand[ops[s]["e"]].append(s)
+    return order
+
+
+def plan(ops, cfg):
+    tm = [times(ops, m) + (m[4],) for m in MODELS]
+    state = [cfg["seed"]]
+
+    def rnd():
+        state[0] = (state[0] * 6364136223846793005 + 1442695040888963407) % (1 << 64)
+        return (state[0] >> 33) / float(1 << 31)
+
+    def score(order):
+        return [max(replay(ops, order, *z)) for z in tm]
+    total = lambda s: 2 * s[0] + s[1] + s[2]
+    n = len(ops)
+    bias = [0.0] * n
+    order = schedule(ops, *tm[0], bias)
+    best = score(order)
+    pick = [k for k, o in enumerate(ops) if o["e"] in "vsg"]
+    same = {}
+    for k, o in enumerate(ops):
+        same.setdefault(o["site"], []).append(k)
+    for _ in range(cfg["iters"]):
+        b = list(bias)
+        for _ in range(1 + int(4 * rnd())):
+            k, d = pick[int(rnd() * len(pick))], (rnd() - 0.5) * (4000.0 if rnd() < 0.3 else 800.0)
+            for j in (same[ops[k]["site"]] if rnd() < 0.5 else [k]):
+                b[j] += d
+        o = schedule(ops, *tm[0], b)
+        s = score(o)
+        if total(s) <= total(best):
+            bias, order, best = b, o, s
+    succ = [[] for _ in range(n)]
+    for k, o in enumerate(ops):
+        for j in o["dep"]:
+            succ[j].append(k)
+    now, top, kept = total(best), total(best), list(order)
+    for it in range(cfg["swaps"]):
+        if it % 8 == 0:
+            c, lat, hop = tm[int(rnd() * len(tm))]
+            fin = replay(ops, order, c, lat, hop)
+            at = {k: i for i, k in enumerate(order)}
+            order.sort(key=lambda k: (fin[k] - c[k] - lat[k], at[k]))
+            prev, lastof = {}, {}
+            for k in order:
+                prev[k] = lastof.get(ops[k]["e"])
+                lastof[ops[k]["e"]] = k
+            pairs, k = [], max(range(n), key=lambda z: fin[z])
+            while k is not None:
+                st, j = fin[k] - c[k] - lat[k], prev[k]
+                nxt = None
+                for d, h in zip(ops[k]["dep"], ops[k]["hop"]):
+                    if abs(fin[d] + h * hop - st) < 1e-6:
+                        nxt = d
+                if nxt is None and j is not None and ops[k]["e"] != "x":
+                    pairs.append((j, k))
+                    nxt = j
+                k = nxt
+        if rnd() < 0.7 and pairs:
+            j, k = pairs[int(rnd() * len(pairs))]
+            while rnd() < 0.4 and prev[j] is not None:
+                j = prev[j]
+        else:
+            k = pick[int(rnd() * len(pick))]
+            j = prev[k]
+            if j is None:
+                continue
+        a, b = order.index(j), order.index(k)
+        if a > b:
+            continue
+        mid = set(order[a:b + 1])
+        if not any(d in mid for d in ops[k]["dep"]) and (rnd() < 0.5 or any(d in mid for d in succ[j])):
+            o = order[:a] + [k] + order[a:b] + order[b + 1:]
+        elif not any(d in mid for d in succ[j]):
+            o = order[:a] + order[a + 1:b + 1] + [j] + order[b + 1:]
+        else:
+            continue
+        s = score(o)
+        if total(s) <= now + cfg["heat"] * (1.0 - it / cfg["swaps"]) * rnd() * rnd():
+            order, now = o, total(s)
+            if now < top:
+                top, kept, best = now, list(o), s
+    return kept, best
+
+
+def emit(g, T, ops, order):
+    queue = {"v": g.vector, "s": g.scalar, "p": g.tensor, "g": g, "y": g.sync}
+    csem = {"v": "cv", "s": "cs", "p": "cp", "g": "cg"}
+    need = set()
+    for o in ops:
+        for j in o["dep"]:
+            if not (ops[j]["e"] == "p" and o["e"] == "p"):
+                need.add(j)
+    clock = {e: {} for e in queue}
+    count = {}
+    mark = {}
+    for k in order:
+        o = ops[k]
+        e = o["e"]
+        if e == "x":
+            mark[k] = (o["sem"][0], o["sem"][1], {})
+            count[o["sem"][0]] = o["sem"][1]
+            continue
+        q, ck = queue[e], clock[e]
+        want = [mark[j] for j in o["dep"] if j in mark and not (ops[j]["e"] == "p" and e == "p")]
+        for (s, v, c) in sorted(want, key=lambda z: -z[1]):
+            if ck.get(s, 0) < v and not any(c2.get(s, 0) >= v and ck.get(s2, 0) < v2 and s2 != s for (s2, v2, c2) in want):
+                q.wait_ge(T.sem[s], v)
+                ck[s] = v
+        for (s, v, c) in want:
+            for s2, v2 in c.items():
+                if ck.get(s2, 0) < v2:
+                    ck[s2] = v2
+        ins = o["fn"](q)
+        if o["k"] == "r":
+            count["sent"] = count.get("sent", 0) + o["sem"]
+        elif o["k"] == "d":
+            ins.then_inc(T.sem[o["sem"]], 16)
+            count[o["sem"]] = 16
+            mark[k] = (o["sem"], 16, dict(ck))
+        elif k in need:
+            s = csem[e]
+            count[s] = count.get(s, 0) + 1
+            ins.then_inc(T.sem[s], 1)
+            mark[k] = (s, count[s], dict(ck))
+    for s, v in count.items():
+        g.wait_ge(T.sem[s], v)
+
+
+def rank_program(g, core, T, topo):
+    rank = T.rank_of(core)
+    if rank is None:
+        return
+    ops = build(T, rank, core, topo, CFG)
+    depend(ops)
+    if "order" not in ORDER:
+        ORDER["order"] = plan(ops, CFG)[0]
+    emit(g, T, ops, ORDER["order"])

@@ -7,24 +7,20 @@ SCRATCH = {
     "af": ("sbuf", [128, 6400], "float32"),
     "ai": ("sbuf", [128, 4608], "int32"),
     "au": ("sbuf", [128, 2304], "uint16"),
-    "pu": ("psum", [128, 512], "float32"),
-    "pk": ("psum", [128, 512], "float32"),
-    "pp": ("psum", [128, 512], "float32"),
-    "pc": ("psum", [128, 512], "float32"),
-    "pr": ("psum", [128, 512], "float32"),
-    "pq": ("psum", [128, 512], "float32"),
 }
+PSUM = ("pu", "pk", "pp", "pc", "pr", "pq", "pv")
+SCRATCH.update({p: ("psum", [128, 512], "float32") for p in PSUM})
 STEPS, V, H = 5, 1024, 2048
 SEMAPHORES = (["cv", "cs", "cp", "cg", "sent", "sig"] + ["d%d" % k for k in range(16)]
               + ["req%d" % t for t in range(STEPS - 1)] + ["rep%d" % t for t in range(STEPS - 1)])
-PSUM = ("pu", "pk", "pp", "pc", "pr", "pq")
 SIZE = {"ab": 2, "af": 4, "ai": 4, "au": 2}
 
-CFG = {"xv": 20, "pv": 28, "iv": 28, "x0": 32, "lastv": 32, "chunks": ((5, "s"), (5, "s"), (4, "s"), (2, "s")),
-       "parts": (16, 16, 16, 16), "on_s": ("b1", "b2", "se2", "sj", "un"), "early": 1, "first": 2500,
-       "iters": 400, "swaps": 10000, "heat": 300.0, "seed": 1}
-MODELS = ((1.0, 1.4, 3.4, 0.75, 80.0, 2200.0, 2300.0), (0.85, 1.0, 1.6, 0.5, 40.0, 1800.0, 1600.0),
-          (1.2, 2.1, 6.0, 1.0, 150.0, 2600.0, 3500.0))
+CFG = {"xv": 28, "pv": 32, "iv": 32, "x0": 32, "lastv": 32, "chunks": (5, 5, 4, 2),
+       "parts": (16, 16, 16, 16), "on_s": ("b1", "b2", "se2", "sj", "un", "dd"), "early": 1, "first": 2500,
+       "iters": 400, "swaps": 16000, "heat": 400.0, "seed": 1}
+MODELS = ((1.04, 1.3, 3.15, 0.9, 200.0, 2200.0, 2300.0), (0.88, 1.0, 1.8, 0.7, 190.0, 2000.0, 1800.0),
+          (1.25, 2.3, 7.0, 1.2, 220.0, 2600.0, 2500.0), (1.1, 1.6, 4.0, 1.0, 220.0, 2800.0, 4400.0))
+ACROSS = 0.6
 ORDER = {}
 
 
@@ -195,12 +191,8 @@ def build(T, rank, core, topo, cfg):
     CWall = new(B_, 192 * STEPS)
     for t in range(STEPS - 1 + cfg["early"]):
         iota(sl(CWall, 192 * t, 192 * t + 192), [[0, 192]], 0)
-    if "se2" in ons:
-        rep16 = new(U_, 16)
-        cp(rep16, sl(io, 0, 16))
-    else:
-        Z2 = new(B_, 256)
-        iota(Z2, [[0, 256]], 0)
+    rep16 = new(U_, 16)
+    cp(rep16, sl(io, 0, 16))
     lane, pF, l4, colb, lane4, c15, cb, c4, cl, hl_ = [col() for _ in range(10)]
     ts(t1, pI, 15, AL.bitwise_and)
     cp(lane, t1)
@@ -235,15 +227,10 @@ def build(T, rank, core, topo, cfg):
     W1, W2 = new(B_, 128), new(B_, 128)
     ts(W1, aB, 8.0, AL.is_lt, sl(wb, 0, 1), AL.mult)
     ts(W2, aB, 8.0, AL.is_lt, sl(wb, 1, 2), AL.mult)
-    who = [w for (_, w) in cfg["chunks"]]
-    Wd, W4 = {}, {}
-    for f in ([-16, 32] if "v" in who else []) + ([16] if "s" in who else []):
-        Wd[f] = new(B_, 144)
-        ts(Wd[f], io, c15, AL.is_equal, float(f), AL.mult)
+    Wd, W4 = new(B_, 144), new(B_, 144)
+    ts(Wd, io, c15, AL.is_equal, 16.0, AL.mult)
     act(a4, io, AF.Abs, bias=c4)
-    for f in ([16] if "r2" in ons else [-16, 32]):
-        W4[f] = new(B_, 144)
-        ts(W4[f], a4, 2.0, AL.is_lt, float(f), AL.mult)
+    ts(W4, a4, 2.0, AL.is_lt, 16.0, AL.mult)
     ts(Id, io128, pF, AL.is_equal)
     Dr = []
     for r in range(4):
@@ -324,17 +311,12 @@ def build(T, rank, core, topo, cfg):
         key = P("pk", 0, 64)
         mm(key, Id, Kw, True, False)
         q0 = 0
-        for n, w in cfg["chunks"]:
+        for n in cfg["chunks"]:
             a, b = 64 * q0, 64 * (q0 + n)
             tt(sl(D, a, b), ind(tagw, sl(hl, 4 * q0, 4 * (q0 + n))), sl(SE, a, b), AL.subtract)
-            if w == "v":
-                ts(sl(R, a, b), sl(D, a, b), 0.0, AL.max)
-                for q in range(q0, q0 + n):
-                    mm(key, sl(Wd[-16], 15 - q, 143 - q), sl(D, 64 * q, 64 * q + 64), False, False)
-            else:
-                act(sl(R, a, b), sl(D, a, b), AF.Abs)
+            act(sl(R, a, b), sl(D, a, b), AF.Abs)
             for q in range(q0, q0 + n):
-                mm(key, sl(Wd[32 if w == "v" else 16], 15 - q, 143 - q), sl(R, 64 * q, 64 * q + 64), False, q == 15)
+                mm(key, sl(Wd, 15 - q, 143 - q), sl(R, 64 * q, 64 * q + 64), False, q == 15)
             q0 += n
         dg, sc, b1, bq = new(F_, 128), new(F_, 128), new(F_, 4), new(F_, 4)
         tt(dg, ind(um, J8), mJ, AL.mult)
@@ -380,14 +362,15 @@ def build(T, rank, core, topo, cfg):
         win = nb
         sJ = new(B_, 64)
         move("sj", sJ, ind(Z, JZ))
-        mm(P("pp", 0, 5), Id, cPos, True, False)
+        mm(P("pp", 0, 4), Id, sl(cPos, 0, 4), True, False)
         mm(P("pp", 0, 4), nL, M, False, False)
         for d in (1, 2, 3):
             mm(P("pp", d, 4), negB, sl(M, 0, 4 - d), False, False)
         for r in range(4):
-            mm(P("pp", r, r + 1), Dr[r], sl(M, r, r + 1), False, False)
+            mm(P("pp", r, r + 1), Dr[r], sl(M, r, r + 1), False, r == 3)
+        mm(P("pv", 0, 1), Id, sl(cPos, 4, 5), True, False)
         for r in range(4):
-            mm(P("pp", 4, 5), negB, sl(M, r, r + 1), False, r == 3)
+            mm(P("pv", 0, 1), negB, sl(M, r, r + 1), False, r == 3)
         posl = new(U_, 4)
         cp(posl, P("pp", 0, 4))
         CW = sl(CWall, 192 * t, 192 * t + 192)
@@ -408,11 +391,7 @@ def build(T, rank, core, topo, cfg):
         mm(P("pr", 32, 48), W2, sL, True, True)
         mm(P("pr", 16, 32), W1, sR, True, True)
         mm(P("pr", 48, 64), W2, sR, True, True)
-        if "se2" in ons:
-            act(SE2, ind(sR, rep16), AF.Copy)
-        else:
-            move("z2", sl(Z2, 0, 256, 16), sR)
-            scan(SE2, sl(keep, 0, 256), Z2, AL.mult, AL.add)
+        move("se2", SE2, ind(sR, rep16))
         vi2, um2, up2, pm2, hl2 = new(I_, 64), new(I_, 64), new(F_, 32), new(I_, 32), new(U_, 16)
         cp(vi2, P("pr", 0, 64))
         ts(um2, vi2, H - 1, AL.bitwise_and)
@@ -423,14 +402,9 @@ def build(T, rank, core, topo, cfg):
         tt(D2, ind(tagw, hl2), SE2, AL.subtract)
         key2 = P("pq", 0, 64)
         mm(key2, Id, K2, True, False)
-        if "r2" in ons:
-            act(R2, D2, AF.Abs)
-        else:
-            ts(R2, D2, 0.0, AL.max)
-            for a in range(4):
-                mm(key2, sl(W4[-16], 12 - 4 * a, 140 - 4 * a), sl(D2, 64 * a, 64 * a + 64), False, False)
+        act(R2, D2, AF.Abs)
         for a in range(4):
-            mm(key2, sl(W4[16 if "r2" in ons else 32], 12 - 4 * a, 140 - 4 * a), sl(R2, 64 * a, 64 * a + 64), False, a == 3)
+            mm(key2, sl(W4, 12 - 4 * a, 140 - 4 * a), sl(R2, 64 * a, 64 * a + 64), False, a == 3)
         dg2, sc2, b2, k2 = new(F_, 48), new(F_, 48), col(), col()
         tt(dg2, sl(um2, 16, 64), sl(mJ, 32, 80), AL.mult)
         scan(sc2, sl(keep, 0, 48), dg2, AL.mult, AL.add)
@@ -440,7 +414,7 @@ def build(T, rank, core, topo, cfg):
         tt(bm, sl(um2, 16, 32), upper, AL.add)
         aff("dd", dd, bm, -1.0, h0c)
         red(mn, dd, AL.min, True)
-        ts(fl, mn, P("pp", 4, 5), AL.min, 0.0, AL.is_le)
+        ts(fl, mn, P("pv", 0, 1), AL.min, 0.0, AL.is_le)
         ts(wl, fl, dum, AL.mult, h0c, AL.max)
         cp(ind(tag, wl), sL)
         red(k2, key2, AL.min)
@@ -479,7 +453,8 @@ def depend(ops):
                 h.append((k, isw, r[1], r[2]))
         dep.discard(k)
         o["dep"] = sorted(dep)
-        o["hop"] = [0 if (ops[j]["e"] == "p" and o["e"] == "p") or o["e"] == "x" else 1 for j in o["dep"]]
+        o["hop"] = [0 if (ops[j]["e"] == "p" and o["e"] == "p") or o["e"] == "x" else (1 if ops[j]["e"] == o["e"] else ACROSS)
+                    for j in o["dep"]]
 
 
 def times(ops, m):
@@ -552,7 +527,7 @@ def plan(ops, cfg):
 
     def score(order):
         return [max(replay(ops, order, *z)) for z in tm]
-    total = lambda s: 2 * s[0] + s[1] + s[2]
+    total = lambda s: s[0] + sum(s)
     n = len(ops)
     bias = [0.0] * n
     order = schedule(ops, *tm[0], bias)

@@ -3,22 +3,23 @@ from concourse.mybir import AluOpType, AxisListType, ActivationFunctionType
 AL = AluOpType
 AF = ActivationFunctionType
 SCRATCH = {
-    "ab": ("sbuf", [128, 23552], "bfloat16"),
-    "af": ("sbuf", [128, 6400], "float32"),
-    "ai": ("sbuf", [128, 4608], "int32"),
-    "au": ("sbuf", [128, 2304], "uint16"),
+    "ab": ("sbuf", [128, 24576], "bfloat16"),
+    "af": ("sbuf", [128, 8192], "float32"),
+    "ai": ("sbuf", [128, 5120], "int32"),
+    "au": ("sbuf", [128, 2560], "uint16"),
 }
-PSUM = ("pu", "pk", "pp", "pc", "pr", "pq", "pv")
+PSUM = ("pu", "pw", "pk", "pp", "pc", "pr", "ps", "pq")
 SCRATCH.update({p: ("psum", [128, 512], "float32") for p in PSUM})
 STEPS, V, H = 5, 1024, 2048
 SEMAPHORES = (["cv", "cs", "cp", "cg", "sent", "sig"] + ["d%d" % k for k in range(16)]
               + ["req%d" % t for t in range(STEPS - 1)] + ["rep%d" % t for t in range(STEPS - 1)])
 SIZE = {"ab": 2, "af": 4, "ai": 4, "au": 2}
 
-CFG = {"xv": 28, "pv": 32, "iv": 32, "x0": 32, "lastv": 32, "chunks": (5, 5, 4, 2),
-       "parts": (16, 16, 16, 16), "on_s": ("b1", "b2", "se2", "sj", "un", "dd"), "early": 1, "first": 2500,
-       "iters": 400, "swaps": 16000, "heat": 400.0, "seed": 1}
-MODELS = ((1.04, 1.3, 3.15, 0.9, 200.0, 2200.0, 2300.0), (0.88, 1.0, 1.8, 0.7, 190.0, 2000.0, 1800.0),
+CFG = {"sites": ((0, 28, "v"), (28, 64, "s")), "sites0": ((0, 32, "v"), (32, 64, "s")), "hash": (64,), "spe": 1,
+       "pv": 32, "iv": 32, "lastv": 32, "chunks": ((5, "a"), (5, "a"), (4, "a"), (2, "a")),
+       "parts": (16, 16, 16, 16), "on_s": ("se2", "h0c", "eq"), "merge": 1, "early": 1, "first": 2500,
+       "exact": 1, "iters": 300, "swaps": 12000, "heat": 400.0, "seed": 1}
+MODELS = ((1.04, 1.3, 3.15, 0.9, 200.0, 2200.0, 2300.0), (0.88, 1.0, 1.8, 0.5, 190.0, 2000.0, 1800.0),
           (1.25, 2.3, 7.0, 1.2, 220.0, 2600.0, 2500.0), (1.1, 1.6, 4.0, 1.0, 220.0, 2800.0, 4400.0))
 ACROSS = 0.6
 ORDER = {}
@@ -55,7 +56,7 @@ def build(T, rank, core, topo, cfg):
     def val(x):
         return ap(x) if isinstance(x, tuple) else x
 
-    def add(eng, fn, ins, out, cost, kind="c", lat=(0, 0, 0), after=(), sem=None):
+    def add(eng, fn, ins, out, cost, kind="c", lat=(0, 0, 0), after=(), sem=None, out2=None):
         rd, wr = [], []
         for x in ins:
             if isinstance(x, tuple):
@@ -65,6 +66,8 @@ def build(T, rank, core, topo, cfg):
                 wr, rd = [out[1]], rd + [out[2]]
             else:
                 wr = [out]
+        if out2 is not None:
+            wr.append(out2)
         site[0] += 1
         ops.append({"site": site[0], "e": eng, "fn": fn, "r": rd, "w": wr, "c": cost, "k": kind, "lat": lat,
                     "after": list(after), "sem": sem})
@@ -97,38 +100,24 @@ def build(T, rank, core, topo, cfg):
         f = 1 if a[0] in PSUM or b[0] in PSUM else 2
         return add("v", lambda q: q.tensor_tensor(ap(out), ap(a), ap(b), o), [a, b], out, size(out, [a], f))
 
-    def scan(out, a, b, o0, o1):
+    def scan(out, a, b, o0, o1, first=0.0):
         f = 0.5 if two([out, a, b]) else 1
-        return add("v", lambda q: q.tensor_tensor_scan(ap(out), ap(a), ap(b), 0.0, o0, o1), [a, b], out, size(out, [a], f))
+        return add("v", lambda q: q.tensor_tensor_scan(ap(out), ap(a), ap(b), first, o0, o1), [a, b], out, size(out, [a], f))
 
-    def red(out, a, o, absv=False):
-        return add("v", lambda q: q.tensor_reduce(ap(out), ap(a), AxisListType.X, o, apply_absolute_value=absv),
-                   [a], out, size(out, [a], 1))
+    def red(out, a, o):
+        return add("v", lambda q: q.tensor_reduce(ap(out), ap(a), AxisListType.X, o), [a], out, size(out, [a], 1))
 
     def ms(out, c):
         return add("v", lambda q: q.memset(ap(out), c), [], out, size(out, [], 0.5 if two([out]) else 1))
 
-    def act(out, a, func=AF.Identity, bias=None, scale=None):
-        kw = {}
-        if bias is not None:
-            kw["bias"] = bias
-        if scale is not None:
-            kw["scale"] = scale
+    def act(out, a, func=AF.Identity, bias=None, scale=None, total=None):
+        kw = {k: x for k, x in (("bias", bias), ("scale", scale), ("accum_out", total)) if x is not None}
         return add("s", lambda q: q.activation(ap(out), ap(a), func, **{k: val(x) for k, x in kw.items()}),
-                   [a, bias, scale], out, size(out, [a], 1, 15))
-
-    def aff(name, out, a, scale, bias):
-        if name in ons:
-            return act(out, a, AF.Identity, bias, scale)
-        if bias is None:
-            return ts(out, a, scale, AL.mult)
-        return ts(out, a, scale, AL.mult, bias, AL.add)
-
-    def move(name, out, a):
-        return act(out, a, AF.Copy) if name in ons else cp(out, a)
+                   [a, bias, scale], out, size(out, [a], 1, 35 if total else 15), out2=total)
 
     def mm(out, l, r, start, stop):
-        return add("p", lambda q: q.matmul(ap(out), ap(l), ap(r), start, stop), [l, r], out, (0, 0, 0, 0, max(64, nel(r))))
+        n = max(64, nel(r)) * (4 if l[0] == "af" else 1)
+        return add("p", lambda q: q.matmul(ap(out), ap(l), ap(r), start, stop), [l, r], out, (0, 0, 0, 0, n))
 
     def iota(out, pat, base, cm=0):
         if out[0] == "ai":
@@ -154,9 +143,12 @@ def build(T, rank, core, topo, cfg):
         nr.append(k)
         return add("x", None, [], land, (0, 0, 0, 0, 0), "x", (0, 0, 1), [k], (sem, n))
 
-    def wide(out, win, lst, nv):
-        cp(sl(out, 0, 16 * nv), ind(win, sl(lst, 0, nv)))
-        act(sl(out, 16 * nv, V), ind(win, sl(lst, nv, 64)), AF.Copy)
+    def gather(e, out, win, lst):
+        return cp(out, ind(win, lst)) if e == "v" else act(out, ind(win, lst), AF.Copy)
+
+    def wide(out, win, lst, parts):
+        for a, b, e in parts:
+            gather(e, sl(out, 16 * a, 16 * b), win, sl(lst, a, b))
 
     B_, F_, I_, U_ = "ab", "af", "ai", "au"
     N = len(T.cores)
@@ -173,14 +165,13 @@ def build(T, rank, core, topo, cfg):
 
     def col():
         return new(F_, 1)
+    BIG = float(1 << 19)
     pI, t1, t2 = new(I_, 1), new(I_, 1), new(I_, 1)
     iota(pI, [[0, 1]], 0, 1)
     io = new(B_, 144)
     iota(io, [[1, 144]], 0)
     Kw = new(B_, 64)
     iota(Kw, [[0, 4], [1, 16]], 0)
-    j8 = new(F_, 8)
-    iota(j8, [[64, 2], [1, 4]], 0)
     bI = new(B_, 64)
     iota(bI, [[1, 4], [0, 16]], 0)
     vals = new(F_, V)
@@ -188,9 +179,9 @@ def build(T, rank, core, topo, cfg):
     iota(sl(vals, 512, V), [[16, 8], [256, 4], [1, 16]], 160)
     cP = new(F_, 64)
     iota(cP, [[256, 4], [1024, 16]], 0)
-    CWall = new(B_, 192 * STEPS)
+    CWall = new(B_, 208 * STEPS)
     for t in range(STEPS - 1 + cfg["early"]):
-        iota(sl(CWall, 192 * t, 192 * t + 192), [[0, 192]], 0)
+        iota(sl(CWall, 208 * t + 176, 208 * t + 192), [[0, 16]], 0)
     rep16 = new(U_, 16)
     cp(rep16, sl(io, 0, 16))
     lane, pF, l4, colb, lane4, c15, cb, c4, cl, hl_ = [col() for _ in range(10)]
@@ -201,16 +192,18 @@ def build(T, rank, core, topo, cfg):
     cp(pF, pI)
     ts(colb, l4, 15.75, AL.mult)
     ts(colb, lane, 0.25, AL.mult, colb, AL.add)
-    baseQ, list0 = new(F_, 4), new(U_, 4)
+    baseQ, list0, base2 = new(F_, 4), new(U_, 4), new(F_, 4)
     ts(baseQ, sl(io, 0, 4), 4.0, AL.mult, colb, AL.add)
     cp(list0, baseQ)
-    KW = 16 * max(32, cfg["xv"], 64 - cfg["xv"], cfg["x0"], 64 - cfg["x0"])
-    keep, reset, Z, rb = new(B_, KW), new(B_, KW), new(B_, V), new(B_, 64)
+    act(base2, baseQ, bias=224.0)
+    KW = max([512] + [16 * (b - a) for a, b, e in cfg["sites"] + cfg["sites0"]])
+    keep, reset, Z, rbA, rbB = new(B_, KW), new(B_, KW), new(B_, V), new(B_, 128), new(B_, 64)
     ms(keep, 1.0)
     ms(sl(keep, 0, KW, 16), 0.0)
     ts(reset, keep, -256.0, AL.mult, 256.0, AL.add)
     ms(Z, 0.0)
-    act(rb, sl(reset, 0, 64), scale=512.0)
+    act(rbA, sl(reset, 0, 128), scale=BIG / 256)
+    act(rbB, sl(keep, 0, 64), scale=2.0 - BIG, bias=BIG)
     ts(c15, lane, -1.0, AL.mult, pF, AL.add)
     ts(c15, c15, 15.0, AL.add)
     act(cb, c15, scale=-1.0, bias=7.5)
@@ -219,59 +212,118 @@ def build(T, rank, core, topo, cfg):
     act(cl, c15, scale=-1.0, bias=hl_)
     act(lane4, lane, scale=4.0)
     io128 = sl(io, 0, 128)
-    aB, aL, a4, negB, Id, nL = new(B_, 128), new(B_, 128), new(B_, 144), new(B_, 128), new(B_, 128), new(B_, 128)
+    aB, aL, a4, negB, Id, nL, hB = [new(B_, 144 if k == 2 else 128) for k in range(7)]
     act(aB, io128, AF.Abs, bias=cb)
     ts(negB, aB, 8.0, AL.is_lt, -1.0, AL.mult)
+    act(hB, negB, scale=0.5)
     act(aL, io128, AF.Abs, bias=cl)
-    ts(nL, aL, hl_, AL.is_le, -1.0, AL.mult)
-    W1, W2 = new(B_, 128), new(B_, 128)
+    ts(nL, aL, hl_, AL.is_le, -0.5, AL.mult)
+    W1, W2, N1, N2 = [new(B_, 128) for _ in range(4)]
     ts(W1, aB, 8.0, AL.is_lt, sl(wb, 0, 1), AL.mult)
     ts(W2, aB, 8.0, AL.is_lt, sl(wb, 1, 2), AL.mult)
+    if cfg["spe"]:
+        act(N1, W1, scale=-1.0)
+        act(N2, W2, scale=-1.0)
     Wd, W4 = new(B_, 144), new(B_, 144)
-    ts(Wd, io, c15, AL.is_equal, 16.0, AL.mult)
+    ts(Wd, io, c15, AL.is_equal, 32.0, AL.mult)
+    if any(m == "r" for n, m in cfg["chunks"]):
+        Wp, Wn = new(B_, 144), new(B_, 144)
+        act(Wp, Wd, scale=2.0)
+        act(Wn, Wd, scale=-1.0)
     act(a4, io, AF.Abs, bias=c4)
-    ts(W4, a4, 2.0, AL.is_lt, 16.0, AL.mult)
+    ts(W4, a4, 2.0, AL.is_lt, 64.0, AL.mult)
     ts(Id, io128, pF, AL.is_equal)
     Dr = []
     for r in range(4):
         cr, d = col(), new(B_, 128)
-        act(cr, lane, bias=65.0 + 16 * r)
+        act(cr, lane, scale=0.5, bias=32.5 + 8 * r)
         act(d, Id, scale=cr)
         Dr.append(d)
-    ones = new(B_, 128)
-    silu = act(ones, sl(keep, 0, 128), AF.Silu, scale=0.0, bias=64.0)
+    of, OFF = col(), new(B_, 128)
+    ts(of, lane, 0.0, AL.is_equal, -0.5, AL.mult)
+    act(of, of, bias=64.0)
+    silu = act(OFF, io128, AF.Silu, scale=0.0, bias=of)
     ops[silu]["c"] = (1300, 128, 0, 0, 0)
-    K2a, K2 = new(B_, 64), new(B_, 64)
-    ts(K2a, bI, l4, AL.not_equal, 65536.0, AL.mult)
-    tt(K2, K2a, Kw, AL.max)
-    cPos = new(B_, 5)
-    act(sl(cPos, 0, 4), sl(io, 0, 4), scale=16.0, bias=lane)
-    act(sl(cPos, 4, 5), lane, scale=-1.0, bias=64.0)
-    J8, JZ = new(U_, 8), new(U_, 4)
-    ts(J8, j8, lane4, AL.add)
-    ts(JZ, sl(j8, 0, 4), lane4, AL.add, 16.0, AL.mult)
-    mJ = new(B_, 128)
-    ts(sl(mJ, 0, 64), Kw, lane, AL.is_equal)
-    act(sl(mJ, 64, 128), sl(mJ, 0, 64), scale=2.0)
-    upper, cadd = new(B_, 16), new(F_, 32)
-    ts(upper, sl(Kw, 0, 16), lane, AL.is_ge, 4096.0, AL.mult)
-    c1, qc, dum, thr, nthr, lane17 = [col() for _ in range(6)]
-    act(c1, lane, scale=64.0, bias=32.0)
-    act(sl(cadd, 0, 16), sl(io, 0, 16), scale=0.0, bias=32.0)
-    act(sl(cadd, 16, 32), sl(io, 0, 16), scale=0.0, bias=c1)
-    act(qc, lane, scale=-1.0, bias=1024.0)
+    twos, ones, K2 = new(F_, 128), new(B_, 64), new(B_, 64)
+    ms(twos, 2.0)
+    ms(ones, 1.0)
+    ts(K2, bI, l4, AL.not_equal, BIG, AL.mult)
+    cPos, nlane = new(B_, 5), col()
+    act(nlane, lane, scale=-1.0, bias=159.0)
+    act(sl(cPos, 0, 4), sl(io, 0, 4), scale=-16.0, bias=nlane)
+    act(sl(cPos, 4, 5), lane, scale=-1.0, bias=-17.0)
+    J8, JZ, dup, offs = new(U_, 8), new(U_, 4), new(U_, 2), new(F_, 2)
+    a, last = 0, None
+    for n in cfg["hash"]:
+        for k, o in ((0, 2 * a + 2 * n), (1, 2 * a + n)):
+            if a == 0:
+                act(sl(offs, k, k + 1), lane4, bias=float(o))
+            else:
+                c = col()
+                ts(c, lane4, float(a), AL.is_ge, float(o - last[k]), AL.mult)
+                tt(sl(offs, k, k + 1), sl(offs, k, k + 1), c, AL.add)
+        last = (2 * a + 2 * n, 2 * a + n)
+        a += n
+    ts(sl(J8, 0, 4), sl(io, 0, 4), sl(offs, 0, 1), AL.add)
+    ts(sl(J8, 4, 8), sl(io, 0, 4), sl(offs, 1, 2), AL.add)
+    ts(JZ, sl(io, 0, 4), lane4, AL.add, 16.0, AL.mult)
+    ts(dup, sl(io, 0, 2), 0.0, AL.mult, lane, AL.add)
+    m0, mJ, MK = new(B_, 64), new(B_, 128), new(B_, 32)
+    ts(m0, Kw, lane, AL.not_equal, BIG / 2, AL.mult)
+    act(sl(mJ, 0, 64), m0, bias=60.0 * H)
+    act(sl(mJ, 64, 128), m0, bias=float(H))
+    ts(sl(MK, 0, 16), sl(Kw, 0, 16), lane, AL.is_le, 4096.0, AL.mult)
+    act(sl(MK, 16, 32), sl(m0, 0, 16), scale=-1.0)
+    c1, dum, thr, nthr, lane17, cidx, zb = [col() for _ in range(7)]
+    act(c1, lane, scale=-64.0, bias=992.0)
+    C1, C2, C0 = new(B_, 128), new(B_, 64), new(B_, 32)
+    act(sl(C1, 0, 64), sl(io, 0, 64), scale=0.0, bias=c1)
+    act(sl(C1, 64, 128), sl(io, 0, 64), scale=0.0)
+    act(sl(C2, 0, 16), sl(io, 0, 16), scale=0.0, bias=32.0)
+    act(sl(C2, 16, 64), sl(C1, 48, 96))
+    if not cfg["merge"]:
+        act(C0, sl(io, 0, 32), scale=0.0)
+        act(sl(C0, 0, 16), sl(C2, 0, 16))
     act(dum, lane, bias=float(H + 1))
-    ts(thr, thi, 16.0, AL.mult, 15.0, AL.add)
-    act(nthr, thr, scale=-float(H))
+    TH = new(F_, 64)
+    ts(thr, thi, 32.0 / BIG, AL.mult)
+    ts(TH, sl(rbA, 0, 64), thr, AL.mult)
+    act(nthr, thr, scale=-BIG, bias=-16.0)
     act(lane17, lane, scale=17.0)
+    ts(cidx, l4, -1.0, AL.mult, lane, AL.add)
+    act(cidx, cidx, scale=16.0, bias=63.0)
+    ts(zb, pF, 0.0, AL.is_equal, -28.0, AL.mult)
     act(sl(ef, H, H + 32), sl(io, 0, 32), scale=0.0, bias=lane17)
     act(sl(tag, H, H + 32), sl(io, 0, 32), scale=0.0)
+    Y = new(F_, 720)
+    stream = lambda i, n=64: sl(Y, 5 + 16 * i, 5 + 16 * i + 5 * n - 4, 5)
+    ends = lambda i, o=0: sl(Y, 80 + o + 16 * i, 80 + o + 16 * i + 241, 80)
+    for i, c in enumerate((0.0, -0.75, -4.0, 1.0)):
+        ms(ends(i, 320), c)
+    c30 = col()
+    act(c30, lane, scale=2.0, bias=-30.0)
+    act(ends(3), sl(io, 0, 4), scale=0.0, bias=c30)
 
     A, MX, MN, SE, D, R, A2, X1 = [new(B_, V) for _ in range(8)]
-    SE2, D2, R2 = new(B_, 256), new(B_, 256), new(B_, 256)
+    SE2, D2, R2, E2, Z2 = [new(B_, 256) for _ in range(5)]
+    if "se2" not in ons:
+        ms(Z2, 0.0)
     W = new(F_, V)
     tagw, efw = sl(tag, 0, H), sl(ef, 0, H + 32)
     P = lambda n, a, b, s=1: (n, a, b, s)
+
+    def hashes(um, n, terms, const, b1, b2):
+        for bank in (b1, b2):
+            mm(P(bank, 0, 2 * n), negB if bank == b1 else Id, sl(OFF, 0, 2 * n) if bank == b1 else const, True, False)
+            for k, (o, wa, wz, rhs) in enumerate(terms):
+                mm(P(bank, o, o + nel(rhs)), wa, rhs, False, False)
+                mm(P(bank, n + o, n + o + nel(rhs)), wz, rhs, False, k == len(terms) - 1)
+        r, pm = new(F_, 2 * n), new(I_, n)
+        ts(r, P(b1, 0, 2 * n), 1.5 * 2 ** 34, AL.add, 1.5 * 2 ** 34, AL.subtract)
+        tt(sl(um, 0, 2 * n), P(b2, 0, 2 * n), r, AL.subtract)
+        tt(pm, sl(um, 0, n), sl(um, n, 2 * n), AL.mult)
+        ts(sl(um, 2 * n, 3 * n), pm, 5, AL.logical_shift_right, H - 1, AL.bitwise_and)
+
     X = X0
     lst, win = list0, nb0
     for t in range(STEPS):
@@ -279,8 +331,8 @@ def build(T, rank, core, topo, cfg):
         site[0] = 1000
         nbl = new(U_, 64)
         cp(nbl, ind(win, lst))
-        xv = cfg["xv"] if t else cfg["x0"]
-        wide(A, X, nbl, xv)
+        segs = cfg["sites"] if t else cfg["sites0"]
+        wide(A, X, nbl, segs)
         w1, w2, nbt = new(I_, 64), new(I_, 64), new(U_, 64)
         ts(w1, nbl, 1025.0, AL.mult)
         ts(w2, w1, 4, AL.logical_shift_right, 1023, AL.bitwise_and)
@@ -292,165 +344,172 @@ def build(T, rank, core, topo, cfg):
         invf, invl = new(F_, 64), new(U_, 64)
         dma("y", lambda o=invf: ap(o), lambda: T[W[0]][0:128:16, W[1]:W[2]], [W], invf, 32768)
         ts(invl, invf, -31.75, AL.add)
-        for a, b in ((0, 16 * xv), (16 * xv, V)):
-            scan(sl(MX, a, b), sl(keep, 0, b - a), sl(A, a, b), AL.mult, AL.max)
-            scan(sl(MN, a, b), sl(reset, 0, b - a), sl(A, a, b), AL.add, AL.min)
-        s = sl(Z, 0, V, 16)
-        tt(s, sl(MX, 15, V, 16), sl(MN, 15, V, 16), AL.subtract)
-        mm(P("pu", 0, 64), W1, s, True, True)
-        mm(P("pu", 64, 128), W2, s, True, True)
-        for a in (0, 512):
-            scan(sl(SE, a, a + 512), sl(keep, 0, 512), sl(Z, a, a + 512), AL.mult, AL.add)
-        ui, um, u1p, pm, hl = new(I_, 128), new(I_, 128), new(F_, 64), new(I_, 64), new(U_, 64)
-        cp(ui, P("pu", 0, 128))
-        ts(um, ui, H - 1, AL.bitwise_and)
-        ts(u1p, sl(um, 0, 64), c1, AL.add)
-        tt(pm, u1p, sl(um, 64, 128), AL.mult)
-        ts(sl(um, 0, 64), pm, 5, AL.logical_shift_right, H - 1, AL.bitwise_and)
-        cp(hl, sl(um, 0, 64))
+        for a, b, e in segs:
+            scan(sl(MX, 16 * a, 16 * b), sl(keep, 0, 16 * (b - a)), sl(A, 16 * a, 16 * b), AL.mult, AL.max)
+            scan(sl(MN, 16 * a, 16 * b), sl(reset, 0, 16 * (b - a)), sl(A, 16 * a, 16 * b), AL.add, AL.min)
+        um, hl = new(I_, 192), new(U_, 64)
+        a = 0
+        for n in cfg["hash"]:
+            b = a + n
+            s, mx, mn = sl(Z, 16 * a, 16 * b, 16), sl(MX, 16 * a + 15, 16 * b, 16), sl(MN, 16 * a + 15, 16 * b, 16)
+            tt(s, mx, mn, AL.subtract)
+            terms = [(0, W1, W2, mx), (0, N1, N2, mn)] if cfg["spe"] else [(0, W1, W2, s)]
+            hashes(sl(um, 3 * a, 3 * b), n, terms, sl(C1, 64 - n, 64 + n), "pu", "pw")
+            cp(sl(hl, a, b), sl(um, 3 * a + 2 * n, 3 * b))
+            for x in range(16 * a, 16 * b, 512):
+                y = min(x + 512, 16 * b)
+                scan(sl(SE, x, y), sl(keep, 0, y - x), sl(Z, x, y), AL.mult, AL.add)
+            a = b
         key = P("pk", 0, 64)
-        mm(key, Id, Kw, True, False)
         q0 = 0
-        for n in cfg["chunks"]:
+        for n, mode in cfg["chunks"]:
             a, b = 64 * q0, 64 * (q0 + n)
             tt(sl(D, a, b), ind(tagw, sl(hl, 4 * q0, 4 * (q0 + n))), sl(SE, a, b), AL.subtract)
-            act(sl(R, a, b), sl(D, a, b), AF.Abs)
+            if mode == "a":
+                act(sl(R, a, b), sl(D, a, b), AF.Abs)
+            else:
+                ts(sl(R, a, b), sl(D, a, b), 0.0, AL.max)
+                for q in range(q0, q0 + n):
+                    mm(key, sl(Wn, 15 - q, 143 - q), sl(D, 64 * q, 64 * q + 64), q == 0, False)
             for q in range(q0, q0 + n):
-                mm(key, sl(Wd, 15 - q, 143 - q), sl(R, 64 * q, 64 * q + 64), False, q == 15)
+                mm(key, sl(Wd if mode == "a" else Wp, 15 - q, 143 - q), sl(R, 64 * q, 64 * q + 64),
+                   q == 0 and mode == "a", q == 15)
             q0 += n
-        dg, sc, b1, bq = new(F_, 128), new(F_, 128), new(F_, 4), new(F_, 4)
-        tt(dg, ind(um, J8), mJ, AL.mult)
-        scan(sc, sl(keep, 0, 128), dg, AL.mult, AL.add)
-        hq, u2q = sl(sc, 15, 64, 16), sl(sc, 79, 128, 16)
-        aff("b1", b1, u2q, qc, None)
-        tt(bq, b1, hq, AL.add)
-        pmn = new(F_, 64)
-        scan(pmn, rb, key, AL.add, AL.min)
-        mk = sl(pmn, 15, 64, 16)
-        ki, mi, tv, vi, wi, un, hb, hbl = [new(I_, 4) for _ in range(5)] + [new(F_, 4), new(F_, 4), new(U_, 4)]
-        if not last:
-            M = new(B_, 4)
-            ts(M, mk, thr, AL.is_le)
-        cp(ki, mk)
-        ts(mi, ki, 15, AL.bitwise_and)
-        tt(tv, mi, u2q, AL.mult)
-        tt(vi, tv, bq, AL.add)
-        ts(wi, vi, H - 1, AL.bitwise_and)
-        aff("un", un, mk, float(H), nthr)
-        tt(hb, wi, un, AL.max)
-        ts(hbl, hb, float(H), AL.min)
+        dg, vi, wi, hbl = new(F_, 128), new(I_, 20), new(I_, 4), new(U_, 4)
+        tt(dg, ind(um, J8), mJ, AL.add)
+        scan(stream(4, 128), rbA, dg, AL.add, AL.min)
+        scan(stream(0), sl(rbA, 0, 64), key, AL.add, AL.min)
+        scan(stream(1), TH, key, AL.max, AL.min)
+        scan(stream(2), rbB, key, AL.add, AL.min)
+        scan(vi, sl(Y, 400, 720, 16), sl(Y, 80, 400, 16), AL.mult, AL.add)
+        ts(wi, sl(vi, 4, 20, 5), 0x7FFC0000 + H - 1, AL.bitwise_and)
+        ts(hbl, wi, float(H), AL.min)
         pf, pl = new(F_, 64), new(U_, 64)
         tt(pf, ind(efw, hbl), cP, AL.add)
         ts(pl, pf, 0.0625, AL.mult, -0.46875, AL.add)
-        wide(A2, A, pl, cfg["lastv"] if last else cfg["pv"])
+        pv = cfg["lastv"] if last else cfg["pv"]
+        wide(A2, A, pl, ((0, pv, "v"), (pv, 64, "s")))
         X = X1
         iv = cfg["lastv"] if last else cfg["iv"]
-        wide(X, A2, invl, iv)
+        wide(X, A2, invl, ((0, iv, "v"), (iv, 64, "s")))
         if last:
             dma("y", lambda: T.y[:, 0:16 * iv], lambda: ap(sl(X1, 0, 16 * iv)), [sl(X1, 0, 16 * iv)], None, 131072)
             dma("s", lambda: T.y[:, 16 * iv:V], lambda: ap(sl(X1, 16 * iv, V)), [sl(X1, 16 * iv, V)], None, 131072)
             break
         site[0] = 2000
-        lm, lb, li, la, lst = new(I_, 4), new(B_, 4), new(I_, 4), new(I_, 4), new(U_, 4)
-        ts(lm, ki, 4, AL.logical_shift_right, 7, AL.bitwise_and)
-        cp(lb, lm)
-        for r in range(4):
-            mm(P("pc", 0, 1), ones, sl(lb, r, r + 1), r == 0, r == 3)
-        ts(li, baseQ, P("pc", 0, 1), AL.add)
-        ts(la, li, 511, AL.bitwise_and)
-        cp(lst, la)
+        kc = ends(0)
+        z, zz, rc, cls, lst = col(), new(F_, 4), col(), col(), new(U_, 4)
+        act(zz, kc, bias=zb, total=z)
+        mm(P("pc", 0, 1), twos, z, True, True)
+        ts(rc, P("pc", 0, 1), 1.5 * 2 ** 32, AL.add, 1.5 * 2 ** 32, AL.subtract)
+        ts(cls, P("pc", 0, 1), rc, AL.subtract)
+        ts(lst, base2, cls, AL.add)
         win = nb
-        sJ = new(B_, 64)
-        move("sj", sJ, ind(Z, JZ))
+        sJ, Sg = new(B_, 64), new(B_, 4)
+        gather("s", sJ, Z, JZ)
+        act(Sg, kc, AF.Sign, bias=nthr)
         mm(P("pp", 0, 4), Id, sl(cPos, 0, 4), True, False)
-        mm(P("pp", 0, 4), nL, M, False, False)
+        mm(P("pp", 0, 4), nL, Sg, False, False)
         for d in (1, 2, 3):
-            mm(P("pp", d, 4), negB, sl(M, 0, 4 - d), False, False)
+            mm(P("pp", d, 4), hB, sl(Sg, 0, 4 - d), False, False)
         for r in range(4):
-            mm(P("pp", r, r + 1), Dr[r], sl(M, r, r + 1), False, r == 3)
-        mm(P("pv", 0, 1), Id, sl(cPos, 4, 5), True, False)
+            mm(P("pp", r, r + 1), Dr[r], sl(Sg, r, r + 1), False, r == 3)
+        mm(P("pc", 0, 1), Id, sl(cPos, 4, 5), True, False)
         for r in range(4):
-            mm(P("pv", 0, 1), negB, sl(M, r, r + 1), False, r == 3)
+            mm(P("pc", 0, 1), hB, sl(Sg, r, r + 1), False, r == 3)
         posl = new(U_, 4)
         cp(posl, P("pp", 0, 4))
-        CW = sl(CWall, 192 * t, 192 * t + 192)
-        cp(ind(CW, posl), sJ)
-        sL = sl(CW, 0, 16)
-        sR, rsrc, rland = new(B_, 16), new(B_, 16), new(B_, 16)
+        CW = sl(CWall, 208 * t, 208 * t + 208)
+        cp(ind(sl(CW, 0, 192), posl), sJ)
+        sL, sR = sl(CW, 176, 192), sl(CW, 192, 208)
+        rland = new(I_, 16)
         hop = 1 + t % (N - 1)
         if t < cfg["early"]:
-            sJR, posR, CR = new(B_, 64), new(U_, 4), sl(CWall, 192 * (STEPS - 1), 192 * STEPS)
+            sJR, posR, CR = new(B_, 64), new(U_, 4), sl(CWall, 208 * (STEPS - 1), 208 * (STEPS - 1) + 192)
             send(sJ, sJR, (rank + hop) % N, "sig")
             send(posl, posR, (rank + hop) % N, "req%d" % t)
             cp(ind(CR, posR), sJR)
-            sR = sl(CR, 0, 16)
+            sR = sl(CR, 176, 192)
         else:
             send(sL, sR, (rank + hop) % N, "req%d" % t)
         site[0] = 3000
-        mm(P("pr", 0, 16), W1, sL, True, True)
-        mm(P("pr", 32, 48), W2, sL, True, True)
-        mm(P("pr", 16, 32), W1, sR, True, True)
-        mm(P("pr", 48, 64), W2, sR, True, True)
-        move("se2", SE2, ind(sR, rep16))
-        vi2, um2, up2, pm2, hl2 = new(I_, 64), new(I_, 64), new(F_, 32), new(I_, 32), new(U_, 16)
-        cp(vi2, P("pr", 0, 64))
-        ts(um2, vi2, H - 1, AL.bitwise_and)
-        tt(up2, sl(um2, 0, 32), cadd, AL.add)
-        tt(pm2, up2, sl(um2, 32, 64), AL.mult)
-        ts(sl(um2, 16, 48), pm2, 5, AL.logical_shift_right, H - 1, AL.bitwise_and)
-        cp(hl2, sl(um2, 32, 48))
+        if cfg["merge"]:
+            um2 = new(I_, 96)
+            terms = [(0, W1, W2, sL), (16, W1, W2, sR)] if t < cfg["early"] else [(0, W1, W2, sl(CW, 176, 208))]
+            hashes(um2, 32, terms, C2, "pr", "ps")
+            h0, hR = sl(um2, 64, 80), sl(um2, 80, 96)
+        else:
+            um2, um3 = new(I_, 48), new(I_, 48)
+            hashes(um2, 16, [(0, W1, W2, sL)], C0, "pr", "ps")
+            hashes(um3, 16, [(0, W1, W2, sR)], sl(C2, 16, 48), "pr", "ps")
+            h0, hR = sl(um2, 32, 48), sl(um3, 32, 48)
+        hl2 = new(U_, 16)
+        cp(hl2, hR)
+        if "se2" in ons:
+            gather("s", SE2, sR, rep16)
+        else:
+            cp(sl(Z2, 0, 256, 16), sR)
+            scan(SE2, sl(keep, 0, 256), Z2, AL.mult, AL.add)
         tt(D2, ind(tagw, hl2), SE2, AL.subtract)
+        gather("s", E2, sl(ef, 0, H), hl2)
         key2 = P("pq", 0, 64)
         mm(key2, Id, K2, True, False)
         act(R2, D2, AF.Abs)
         for a in range(4):
             mm(key2, sl(W4, 12 - 4 * a, 140 - 4 * a), sl(R2, 64 * a, 64 * a + 64), False, a == 3)
-        dg2, sc2, b2, k2 = new(F_, 48), new(F_, 48), col(), col()
-        tt(dg2, sl(um2, 16, 64), sl(mJ, 32, 80), AL.mult)
-        scan(sc2, sl(keep, 0, 48), dg2, AL.mult, AL.add)
-        h0c, hq2, u2q2 = sl(sc2, 15, 16), sl(sc2, 31, 32), sl(sc2, 47, 48)
-        aff("b2", b2, u2q2, qc, hq2)
-        bm, dd, mn, fl, wl = new(F_, 16), new(F_, 16), col(), col(), new(U_, 1)
-        tt(bm, sl(um2, 16, 32), upper, AL.add)
-        aff("dd", dd, bm, -1.0, h0c)
-        red(mn, dd, AL.min, True)
-        ts(fl, mn, P("pv", 0, 1), AL.min, 0.0, AL.is_le)
-        ts(wl, fl, dum, AL.mult, h0c, AL.max)
+        bm, eq, junk, h0c, cnt, wl = new(F_, 32), new(F_, 17), new(F_, 17), col(), col(), new(U_, 1)
+        tt(bm, ind(h0, dup), MK, AL.add)
+        if "h0c" in ons:
+            act(sl(junk, 0, 16), sl(bm, 16, 32), AF.Relu, total=h0c)
+        else:
+            red(h0c, sl(bm, 16, 32), AL.max)
+        if "eq" in ons:
+            act(sl(eq, 16, 17), P("pc", 0, 1), AF.Relu, scale=-1.0)
+            act(sl(eq, 0, 16), sl(bm, 0, 16), AF.Abs, scale=-1.0, bias=h0c)
+            act(new(F_, 17), eq, AF.Relu, scale=-4096.0, bias=4096.0, total=cnt)
+        else:
+            act(sl(eq, 16, 17), P("pc", 0, 1), AF.Relu, scale=4096.0, bias=4096.0)
+            ts(sl(eq, 0, 16), sl(bm, 0, 16), h0c, AL.is_equal, 4096.0, AL.mult)
+            red(cnt, eq, AL.max)
+        ts(wl, cnt, h0c, AL.max, dum, AL.min)
         cp(ind(tag, wl), sL)
+        kb, k2, idx, e1, e2 = new(F_, 64), col(), new(U_, 1), new(I_, 16), new(I_, 16)
+        scan(kb, ones, key2, AL.add, AL.min, BIG)
         red(k2, key2, AL.min)
-        ki2, m2, v2, x2, hb2 = new(I_, 1), new(I_, 1), new(I_, 1), new(I_, 1), new(U_, 1)
-        cp(ki2, k2)
-        ts(m2, ki2, 15, AL.bitwise_and)
-        ts(v2, m2, u2q2, AL.mult, b2, AL.add)
-        ts(x2, v2, H - 1, AL.bitwise_and)
-        cp(hb2, x2)
-        e1, e2 = new(I_, 16), new(I_, 16)
-        ts(e1, ind(efw, hb2), 257.0, AL.mult)
+        ts(idx, k2, sl(kb, 63, 64), AL.subtract, cidx, AL.add)
+        ts(e1, ind(E2, idx), 257.0, AL.mult)
         ts(e2, e1, 4, AL.logical_shift_right, 255, AL.bitwise_and)
-        cp(rsrc, e2)
-        send(rsrc, rland, (rank - hop) % N, "rep%d" % t)
+        send(e2, rland, (rank - hop) % N, "rep%d" % t)
         cp(ind(ef, wl), rland)
     return ops
 
 
-def depend(ops):
+def meet(r, z, exact):
+    if r[2] <= z[1] or z[2] <= r[1]:
+        return False
+    if not exact or (r[3] == 1 and z[3] == 1):
+        return True
+    return not set(range(r[1], r[2], r[3])).isdisjoint(range(z[1], z[2], z[3]))
+
+
+def depend(ops, exact):
     hist = {}
     for k, o in enumerate(ops):
         dep = set(o["after"])
         for isw, rs in ((False, o["r"]), (True, o["w"])):
             for r in rs:
-                for (j, w, a, b) in hist.get(r[0], []):
+                for (j, w, z) in hist.get(r[0], []):
                     if r[0] in PSUM:
                         if ops[j]["e"] != o["e"] or w or isw:
                             dep.add(j)
-                    elif (w or isw) and a < r[2] and r[1] < b:
+                    elif (w or isw) and meet(r, z, exact):
                         dep.add(j)
         for isw, rs in ((False, o["r"]), (True, o["w"])):
             for r in rs:
                 h = hist.setdefault(r[0], [])
                 if isw:
-                    h[:] = [z for z in h if not (r[3] == 1 and r[1] <= z[2] and z[3] <= r[2])]
-                h.append((k, isw, r[1], r[2]))
+                    h[:] = [x for x in h if not (x[2] == r or (r[3] == 1 and r[1] <= x[2][1] and x[2][2] <= r[2]))]
+                h.append((k, isw, r))
         dep.discard(k)
         o["dep"] = sorted(dep)
         o["hop"] = [0 if (ops[j]["e"] == "p" and o["e"] == "p") or o["e"] == "x" else (1 if ops[j]["e"] == o["e"] else ACROSS)
@@ -648,7 +707,7 @@ def rank_program(g, core, T, topo):
     if rank is None:
         return
     ops = build(T, rank, core, topo, CFG)
-    depend(ops)
+    depend(ops, CFG["exact"])
     if "order" not in ORDER:
-        ORDER["order"] = plan(ops, CFG)[0]
+        ORDER["order"], ORDER["best"] = plan(ops, CFG)
     emit(g, T, ops, ORDER["order"])

@@ -3,7 +3,7 @@ from concourse.mybir import AluOpType, AxisListType, ActivationFunctionType
 AL = AluOpType
 AF = ActivationFunctionType
 SCRATCH = {
-    "ab": ("sbuf", [128, 24576], "bfloat16"),
+    "ab": ("sbuf", [128, 28672], "bfloat16"),
     "af": ("sbuf", [128, 8192], "float32"),
     "ai": ("sbuf", [128, 5120], "int32"),
     "au": ("sbuf", [128, 2560], "uint16"),
@@ -11,17 +11,19 @@ SCRATCH = {
 PSUM = ("pu", "pw", "pk", "pp", "pc", "pr", "ps", "pq")
 SCRATCH.update({p: ("psum", [128, 512], "float32") for p in PSUM})
 STEPS, V, H = 5, 1024, 2048
-SEMAPHORES = (["cv", "cs", "cp", "cg", "sent", "sig"] + ["d%d" % k for k in range(16)]
-              + ["req%d" % t for t in range(STEPS - 1)] + ["rep%d" % t for t in range(STEPS - 1)])
+SEMAPHORES = (["cv", "cs", "cp", "cg", "sent", "wt1", "wt2", "wt3"] + ["d%d" % k for k in range(16)]
+              + [s + str(t) for s in ("sig", "req", "rep") for t in range(STEPS - 1)])
 SIZE = {"ab": 2, "af": 4, "ai": 4, "au": 2}
 
-CFG = {"sites": ((0, 28, "v"), (28, 64, "s")), "sites0": ((0, 32, "v"), (32, 64, "s")), "hash": (64,), "spe": 1,
-       "pv": 32, "iv": 32, "lastv": 32, "chunks": ((5, "a"), (5, "a"), (4, "a"), (2, "a")),
-       "parts": (16, 16, 16, 16), "on_s": ("se2", "h0c", "eq"), "merge": 1, "early": 1, "first": 2500,
-       "exact": 1, "iters": 300, "swaps": 12000, "heat": 400.0, "seed": 1}
-MODELS = ((1.04, 1.3, 3.15, 0.9, 200.0, 2200.0, 2300.0), (0.88, 1.0, 1.8, 0.5, 190.0, 2000.0, 1800.0),
-          (1.25, 2.3, 7.0, 1.2, 220.0, 2600.0, 2500.0), (1.1, 1.6, 4.0, 1.0, 220.0, 2800.0, 4400.0))
-ACROSS = 0.6
+CFG = {"sites": ((0, 24, "v"), (24, 46, "s"), (46, 64, "s")), "sites0": ((0, 32, "v"), (32, 64, "s")),
+       "slots": ((0, 28, "v"), (28, 64, "s")), "back": ((0, 32, "v"), (32, 64, "s")),
+       "out": ((0, 20, "v"), (20, 32, "v"), (32, 52, "s"), (52, 64, "s")), "spread": (512, 512),
+       "chunks": ((0, 5, "a"), (5, 5, "a"), (10, 4, "a"), (14, 2, "a")),
+       "parts": (12, 12, 12, 12, 8, 8), "on_s": ("s", "r2", "e2", "h0c", "eq"), "first": 2500, "deal": (64,), "home": 0, "far": 0,
+       "exact": 1, "iters": 100, "swaps": 140000, "heat": 2500.0, "mean": 0.5, "joint": 0.5, "long": 0.5, "ahead": 0.0, "seed": 1}
+MODELS = ((0.85, 1.3, 3.15, 0.65, 200.0, 1800.0, 2300.0, 1.0), (1.0, 1.6, 3.9, 0.8, 200.0, 2000.0, 2600.0, 0.9),
+          (1.25, 2.3, 7.0, 0.9, 220.0, 2400.0, 2600.0, 0.6), (1.0, 1.3, 2.5, 0.9, 250.0, 2400.0, 3500.0, 0.8))
+ACROSS = 1.0
 ORDER = {}
 
 
@@ -133,15 +135,15 @@ def build(T, rank, core, topo, cfg):
         nd[0] += 1
         return add(eng, lambda q: q.dma_start(fo(), fi()), ins, out, (60, 0, 0, 0, 0), "d", (nbytes / 200.0, 1, 0), after, s)
 
-    def send(src, land, dst_rank, sem):
+    def send(src, land, dst_rank, sem, more=0):
         dst = T.cores[dst_rank]
         rid, pid = topo.addr(dst, core)
         m = topo.mask(core, dst)
         n = len(topo.engines(core, dst))
         k = add("g", lambda q: q.remote_dma(ap(land), ap(src), T.sem[sem], T.sem.sent, pid, rid, m), [src], None,
-                (300 + (0 if nr else cfg["first"]), 0, 0, 0, 0), "r", sem=n)
+                (300 + (0 if nr else cfg["first"]), 0, 0, 0, 0), "r", after=nr[:1], sem=n)
         nr.append(k)
-        return add("x", None, [], land, (0, 0, 0, 0, 0), "x", (0, 0, 1), [k], (sem, n))
+        return add("x", None, [], land, (0, 0, 0, 0, 0), "x", (more, 0, 1), [k], (sem, n))
 
     def gather(e, out, win, lst):
         return cp(out, ind(win, lst)) if e == "v" else act(out, ind(win, lst), AF.Copy)
@@ -158,9 +160,9 @@ def build(T, rank, core, topo, cfg):
     k0 = dma("y", lambda: ap(nb0), lambda: T.nb[:, 64 * c0:64 * c0 + 64], [], nb0, 32768)
     kx = dma("s", lambda: ap(X0), lambda: T.x[:], [], X0, 262144)
     dma("s", lambda: ap(wb), lambda: T.w[:], [], wb, 262144)
+    dma("s", lambda: ap(thi), lambda: T.th[:], [], thi, 262144)
     dma("y", lambda: ap(sl(tag, 0, H)), lambda: T.tag[:], [], sl(tag, 0, H), 786432)
     dma("y", lambda: ap(sl(ef, 0, H)), lambda: T.ef[:], [], sl(ef, 0, H), 786432, [k0])
-    dma("y", lambda: ap(thi), lambda: T.th[:], [], thi, 786432, [k0])
     dma("y", lambda: ap(nb), lambda: T.nb[:], [], nb, 786432, [kx])
 
     def col():
@@ -179,11 +181,14 @@ def build(T, rank, core, topo, cfg):
     iota(sl(vals, 512, V), [[16, 8], [256, 4], [1, 16]], 160)
     cP = new(F_, 64)
     iota(cP, [[256, 4], [1024, 16]], 0)
-    CWall = new(B_, 208 * STEPS)
-    for t in range(STEPS - 1 + cfg["early"]):
-        iota(sl(CWall, 208 * t + 176, 208 * t + 192), [[0, 16]], 0)
-    rep16 = new(U_, 16)
-    cp(rep16, sl(io, 0, 16))
+    CW = new(B_, 16 * 192)
+    iota(sl(CW, 16 * 176, 16 * 192), [[0, 256]], 0)
+    if "sq" in ons:
+        rep16 = new(U_, 16)
+        cp(rep16, sl(io, 0, 16))
+    elif not cfg["far"]:
+        Z2 = new(B_, 256)
+        iota(Z2, [[0, 256]], 0)
     lane, pF, l4, colb, lane4, c15, cb, c4, cl, hl_ = [col() for _ in range(10)]
     ts(t1, pI, 15, AL.bitwise_and)
     cp(lane, t1)
@@ -192,10 +197,13 @@ def build(T, rank, core, topo, cfg):
     cp(pF, pI)
     ts(colb, l4, 15.75, AL.mult)
     ts(colb, lane, 0.25, AL.mult, colb, AL.add)
-    baseQ, list0, base2 = new(F_, 4), new(U_, 4), new(F_, 4)
-    ts(baseQ, sl(io, 0, 4), 4.0, AL.mult, colb, AL.add)
-    cp(list0, baseQ)
-    act(base2, baseQ, bias=224.0)
+    list0, turn = new(U_, 4), new(F_, 15)
+    ts(list0, sl(io, 0, 4), 4.0, AL.mult, colb, AL.add)
+    ms(turn, 1.0)
+    ms(sl(turn, 7, 8), -1.0)
+    for a, b, c in ((4, 5, -224.0), (5, 6, 1.5 * 2 ** 32), (6, 7, -1.5 * 2 ** 32), (12, 15, 4.0)):
+        ms(("pc", a, b, 1), c)
+    cp(("pc", 11, 12, 1), colb)
     KW = max([512] + [16 * (b - a) for a, b, e in cfg["sites"] + cfg["sites0"]])
     keep, reset, Z, rbA, rbB = new(B_, KW), new(B_, KW), new(B_, V), new(B_, 128), new(B_, 64)
     ms(keep, 1.0)
@@ -215,28 +223,39 @@ def build(T, rank, core, topo, cfg):
     aB, aL, a4, negB, Id, nL, hB = [new(B_, 144 if k == 2 else 128) for k in range(7)]
     act(aB, io128, AF.Abs, bias=cb)
     ts(negB, aB, 8.0, AL.is_lt, -1.0, AL.mult)
-    act(hB, negB, scale=0.5)
+    act(hB, negB, scale=8.0)
     act(aL, io128, AF.Abs, bias=cl)
-    ts(nL, aL, hl_, AL.is_le, -0.5, AL.mult)
+    ts(nL, aL, hl_, AL.is_le, -8.0, AL.mult)
     W1, W2, N1, N2 = [new(B_, 128) for _ in range(4)]
     ts(W1, aB, 8.0, AL.is_lt, sl(wb, 0, 1), AL.mult)
     ts(W2, aB, 8.0, AL.is_lt, sl(wb, 1, 2), AL.mult)
-    if cfg["spe"]:
-        act(N1, W1, scale=-1.0)
-        act(N2, W2, scale=-1.0)
+    WR = {}
+    for hop in range(1, N):
+        wr, WR[hop] = new(B_, 2), (new(B_, 128), new(B_, 128))
+        send(wb, wr, (rank - hop) % N, "wt%d" % hop)
+        for k in range(2):
+            ts(WR[hop][k], aB, 8.0, AL.is_lt, sl(wr, k, k + 1), AL.mult)
+    act(N1, W1, scale=-1.0)
+    act(N2, W2, scale=-1.0)
     Wd, W4 = new(B_, 144), new(B_, 144)
     ts(Wd, io, c15, AL.is_equal, 32.0, AL.mult)
-    if any(m == "r" for n, m in cfg["chunks"]):
+    if any(m in "rx" for q, n, m in cfg["chunks"]):
         Wp, Wn = new(B_, 144), new(B_, 144)
         act(Wp, Wd, scale=2.0)
         act(Wn, Wd, scale=-1.0)
     act(a4, io, AF.Abs, bias=c4)
     ts(W4, a4, 2.0, AL.is_lt, 64.0, AL.mult)
+    if "r2" not in ons:
+        W4p, W4n = new(B_, 144), new(B_, 144)
+        act(W4p, W4, scale=2.0)
+        act(W4n, W4, scale=-1.0)
     ts(Id, io128, pF, AL.is_equal)
+    nId = new(B_, 128)
+    act(nId, Id, scale=-1.0)
     Dr = []
     for r in range(4):
         cr, d = col(), new(B_, 128)
-        act(cr, lane, scale=0.5, bias=32.5 + 8 * r)
+        act(cr, lane, scale=8.0, bias=16 * (32.5 + 8 * r))
         act(d, Id, scale=cr)
         Dr.append(d)
     of, OFF = col(), new(B_, 128)
@@ -249,23 +268,12 @@ def build(T, rank, core, topo, cfg):
     ms(ones, 1.0)
     ts(K2, bI, l4, AL.not_equal, BIG, AL.mult)
     cPos, nlane = new(B_, 5), col()
-    act(nlane, lane, scale=-1.0, bias=159.0)
-    act(sl(cPos, 0, 4), sl(io, 0, 4), scale=-16.0, bias=nlane)
-    act(sl(cPos, 4, 5), lane, scale=-1.0, bias=-17.0)
-    J8, JZ, dup, offs = new(U_, 8), new(U_, 4), new(U_, 2), new(F_, 2)
-    a, last = 0, None
-    for n in cfg["hash"]:
-        for k, o in ((0, 2 * a + 2 * n), (1, 2 * a + n)):
-            if a == 0:
-                act(sl(offs, k, k + 1), lane4, bias=float(o))
-            else:
-                c = col()
-                ts(c, lane4, float(a), AL.is_ge, float(o - last[k]), AL.mult)
-                tt(sl(offs, k, k + 1), sl(offs, k, k + 1), c, AL.add)
-        last = (2 * a + 2 * n, 2 * a + n)
-        a += n
-    ts(sl(J8, 0, 4), sl(io, 0, 4), sl(offs, 0, 1), AL.add)
-    ts(sl(J8, 4, 8), sl(io, 0, 4), sl(offs, 1, 2), AL.add)
+    act(nlane, lane, scale=-16.0, bias=16 * 159.0)
+    act(sl(cPos, 0, 4), sl(io, 0, 4), scale=-256.0, bias=nlane)
+    act(sl(cPos, 4, 5), lane, scale=-16.0, bias=-16 * 17.0)
+    J8, JZ, dup = new(U_, 8), new(U_, 4), new(U_, 2)
+    ts(sl(J8, 0, 4), sl(io, 64, 68), lane4, AL.add)
+    ts(sl(J8, 4, 8), sl(io, 0, 4), lane4, AL.add)
     ts(JZ, sl(io, 0, 4), lane4, AL.add, 16.0, AL.mult)
     ts(dup, sl(io, 0, 2), 0.0, AL.mult, lane, AL.add)
     m0, mJ, MK = new(B_, 64), new(B_, 128), new(B_, 32)
@@ -276,14 +284,11 @@ def build(T, rank, core, topo, cfg):
     act(sl(MK, 16, 32), sl(m0, 0, 16), scale=-1.0)
     c1, dum, thr, nthr, lane17, cidx, zb = [col() for _ in range(7)]
     act(c1, lane, scale=-64.0, bias=992.0)
-    C1, C2, C0 = new(B_, 128), new(B_, 64), new(B_, 32)
+    C1, C2 = new(B_, 128), new(B_, 64)
     act(sl(C1, 0, 64), sl(io, 0, 64), scale=0.0, bias=c1)
     act(sl(C1, 64, 128), sl(io, 0, 64), scale=0.0)
     act(sl(C2, 0, 16), sl(io, 0, 16), scale=0.0, bias=32.0)
     act(sl(C2, 16, 64), sl(C1, 48, 96))
-    if not cfg["merge"]:
-        act(C0, sl(io, 0, 32), scale=0.0)
-        act(sl(C0, 0, 16), sl(C2, 0, 16))
     act(dum, lane, bias=float(H + 1))
     TH = new(F_, 64)
     ts(thr, thi, 32.0 / BIG, AL.mult)
@@ -292,7 +297,6 @@ def build(T, rank, core, topo, cfg):
     act(lane17, lane, scale=17.0)
     ts(cidx, l4, -1.0, AL.mult, lane, AL.add)
     act(cidx, cidx, scale=16.0, bias=63.0)
-    ts(zb, pF, 0.0, AL.is_equal, -28.0, AL.mult)
     act(sl(ef, H, H + 32), sl(io, 0, 32), scale=0.0, bias=lane17)
     act(sl(tag, H, H + 32), sl(io, 0, 32), scale=0.0)
     Y = new(F_, 720)
@@ -300,15 +304,14 @@ def build(T, rank, core, topo, cfg):
     ends = lambda i, o=0: sl(Y, 80 + o + 16 * i, 80 + o + 16 * i + 241, 80)
     for i, c in enumerate((0.0, -0.75, -4.0, 1.0)):
         ms(ends(i, 320), c)
-    c30 = col()
+    c30, part = col(), col()
+    act(part, lane, scale=0.0625, bias=128.0 - 15.0 / 32)
     act(c30, lane, scale=2.0, bias=-30.0)
     act(ends(3), sl(io, 0, 4), scale=0.0, bias=c30)
 
     A, MX, MN, SE, D, R, A2, X1 = [new(B_, V) for _ in range(8)]
-    SE2, D2, R2, E2, Z2 = [new(B_, 256) for _ in range(5)]
-    if "se2" not in ons:
-        ms(Z2, 0.0)
-    W = new(F_, V)
+    D2, R2, E2 = [new(B_, 256) for _ in range(3)]
+    WW = (new(F_, V), new(F_, V))
     tagw, efw = sl(tag, 0, H), sl(ef, 0, H + 32)
     P = lambda n, a, b, s=1: (n, a, b, s)
 
@@ -320,11 +323,15 @@ def build(T, rank, core, topo, cfg):
                 mm(P(bank, n + o, n + o + nel(rhs)), wz, rhs, False, k == len(terms) - 1)
         r, pm = new(F_, 2 * n), new(I_, n)
         ts(r, P(b1, 0, 2 * n), 1.5 * 2 ** 34, AL.add, 1.5 * 2 ** 34, AL.subtract)
-        tt(sl(um, 0, 2 * n), P(b2, 0, 2 * n), r, AL.subtract)
-        tt(pm, sl(um, 0, n), sl(um, n, 2 * n), AL.mult)
+        if n > 32:
+            tt(P(b1, 256, 256 + n), P(b2, 0, n), sl(r, 0, n), AL.subtract)
+            tt(sl(um, n, 2 * n), P(b2, n, 2 * n), sl(r, n, 2 * n), AL.subtract)
+            tt(pm, P(b1, 256, 256 + n), sl(um, n, 2 * n), AL.mult)
+        else:
+            tt(sl(um, 0, 2 * n), P(b2, 0, 2 * n), r, AL.subtract)
+            tt(pm, sl(um, 0, n), sl(um, n, 2 * n), AL.mult)
         ts(sl(um, 2 * n, 3 * n), pm, 5, AL.logical_shift_right, H - 1, AL.bitwise_and)
 
-    X = X0
     lst, win = list0, nb0
     for t in range(STEPS):
         last = t == STEPS - 1
@@ -332,51 +339,91 @@ def build(T, rank, core, topo, cfg):
         nbl = new(U_, 64)
         cp(nbl, ind(win, lst))
         segs = cfg["sites"] if t else cfg["sites0"]
-        wide(A, X, nbl, segs)
-        w1, w2, nbt = new(I_, 64), new(I_, 64), new(U_, 64)
-        ts(w1, nbl, 1025.0, AL.mult)
-        ts(w2, w1, 4, AL.logical_shift_right, 1023, AL.bitwise_and)
-        cp(nbt, w2)
-        a = 0
+        home = last or cfg["home"]
+        if t and cfg["home"]:
+            site[0] = 1050
+            wide(A, X1, nbl, segs)
+        elif t:
+            for a, b, e in cfg["back"]:
+                if e == "v":
+                    ts(sl(X1, 16 * a, 16 * b), ind(W, sl(nbl, a, b)), 0.0625, AL.mult, part, AL.add)
+                else:
+                    act(sl(X1, 16 * a, 16 * b), ind(W, sl(nbl, a, b)), scale=0.0625, bias=part)
+            site[0] = 1010
+            at, a = new(U_, 64), 0
+            for n, bank in zip(cfg["deal"], ("pk", "pq")):
+                for k in range(16):
+                    mm(P(bank, 0, n), sl(Wd, 15 - k, 143 - k), sl(X1, 16 * a + k, 16 * (a + n), 16), k == 0, k == 15)
+                ts(sl(at, a, a + n), P(bank, 0, n), 1.0 / 32, AL.mult, -2080.0, AL.add)
+                a += n
+            site[0] = 1050
+            wide(A, A2, at, segs)
+        else:
+            site[0] = 1050
+            wide(A, X0, nbl, segs)
+        nbt, site[0] = nbl, 1060
+        if home:
+            w1, w2, nbt = new(I_, 64), new(I_, 64), new(U_, 64)
+            ts(w1, nbl, 1025.0, AL.mult)
+            ts(w2, w1, 4, AL.logical_shift_right, 1023, AL.bitwise_and)
+            cp(nbt, w2)
+        a, W, site[0] = 0, WW[t % 2], 1070
         for n in cfg["parts"]:
             ops[act(ind(W, sl(nbt, a, a + n)), sl(vals, 16 * a, 16 * (a + n)), AF.Silu)]["after"].append(silu)
             a += n
-        invf, invl = new(F_, 64), new(U_, 64)
-        dma("y", lambda o=invf: ap(o), lambda: T[W[0]][0:128:16, W[1]:W[2]], [W], invf, 32768)
-        ts(invl, invf, -31.75, AL.add)
+        if home:
+            invf, invl = new(F_, 64), new(U_, 64)
+            dma("y", lambda o=invf: ap(o), lambda W=W: T[W[0]][0:128:16, W[1]:W[2]], [W], invf, 32768)
+            ts(invl, invf, -31.75, AL.add)
+        site[0] = 1090
         for a, b, e in segs:
             scan(sl(MX, 16 * a, 16 * b), sl(keep, 0, 16 * (b - a)), sl(A, 16 * a, 16 * b), AL.mult, AL.max)
             scan(sl(MN, 16 * a, 16 * b), sl(reset, 0, 16 * (b - a)), sl(A, 16 * a, 16 * b), AL.add, AL.min)
-        um, hl = new(I_, 192), new(U_, 64)
-        a = 0
-        for n in cfg["hash"]:
-            b = a + n
-            s, mx, mn = sl(Z, 16 * a, 16 * b, 16), sl(MX, 16 * a + 15, 16 * b, 16), sl(MN, 16 * a + 15, 16 * b, 16)
+        um, hl, site[0] = new(I_, 192), new(U_, 64), 1100
+        s, mx, mn = sl(Z, 0, V, 16), sl(MX, 15, V, 16), sl(MN, 15, V, 16)
+        hashes(um, 64, [(0, W1, W2, mx), (0, N1, N2, mn)], C1, "pu", "pw")
+        cp(hl, sl(um, 128, 192))
+        if "s" in ons:
+            mm(P("pp", 0, 64), Id, mx, True, False)
+            mm(P("pp", 0, 64), nId, mn, False, True)
+            act(s, P("pp", 0, 64))
+        else:
             tt(s, mx, mn, AL.subtract)
-            terms = [(0, W1, W2, mx), (0, N1, N2, mn)] if cfg["spe"] else [(0, W1, W2, s)]
-            hashes(sl(um, 3 * a, 3 * b), n, terms, sl(C1, 64 - n, 64 + n), "pu", "pw")
-            cp(sl(hl, a, b), sl(um, 3 * a + 2 * n, 3 * b))
-            for x in range(16 * a, 16 * b, 512):
-                y = min(x + 512, 16 * b)
-                scan(sl(SE, x, y), sl(keep, 0, y - x), sl(Z, x, y), AL.mult, AL.add)
-            a = b
-        key = P("pk", 0, 64)
-        q0 = 0
-        for n, mode in cfg["chunks"]:
+        a = 0
+        for n in cfg["spread"]:
+            scan(sl(SE, a, a + n), sl(keep, 0, n), sl(Z, a, a + n), AL.mult, AL.add)
+            a += n
+        key, begun = P("pk", 0, 64), []
+
+        def sums(sel, src, q0, n, stop=False):
+            for q in range(q0, q0 + n):
+                mm(key, sl(sel, 15 - q, 143 - q), sl(src, 64 * q, 64 * q + 64), not begun, stop and q == q0 + n - 1)
+                begun.append(q)
+        for q0, n, mode in cfg["chunks"]:
+            if mode == "x":
+                sums(Wn, SE, q0, n)
+        for k, (q0, n, mode) in enumerate(cfg["chunks"]):
             a, b = 64 * q0, 64 * (q0 + n)
-            tt(sl(D, a, b), ind(tagw, sl(hl, 4 * q0, 4 * (q0 + n))), sl(SE, a, b), AL.subtract)
+            lst4 = sl(hl, 4 * q0, 4 * (q0 + n))
+            if mode == "p":
+                mm(P("ps", 0, b - a), nId, sl(SE, a, b), True, False)
+                gather("s", sl(D, a, b), tagw, lst4)
+                mm(P("ps", 0, b - a), Id, sl(D, a, b), False, True)
+                act(sl(R, a, b), P("ps", 0, b - a), AF.Abs)
+            elif mode == "x":
+                gather("s", sl(D, a, b), tagw, lst4)
+                tt(sl(R, a, b), ind(tagw, lst4), sl(SE, a, b), AL.max)
+            else:
+                tt(sl(D, a, b), ind(tagw, lst4), sl(SE, a, b), AL.subtract)
             if mode == "a":
                 act(sl(R, a, b), sl(D, a, b), AF.Abs)
-            else:
+            if mode == "r":
                 ts(sl(R, a, b), sl(D, a, b), 0.0, AL.max)
-                for q in range(q0, q0 + n):
-                    mm(key, sl(Wn, 15 - q, 143 - q), sl(D, 64 * q, 64 * q + 64), q == 0, False)
-            for q in range(q0, q0 + n):
-                mm(key, sl(Wd if mode == "a" else Wp, 15 - q, 143 - q), sl(R, 64 * q, 64 * q + 64),
-                   q == 0 and mode == "a", q == 15)
-            q0 += n
+            if mode in "rx":
+                sums(Wn, D, q0, n)
+            sums(Wp if mode in "rx" else Wd, R, q0, n, k == len(cfg["chunks"]) - 1)
         dg, vi, wi, hbl = new(F_, 128), new(I_, 20), new(I_, 4), new(U_, 4)
-        tt(dg, ind(um, J8), mJ, AL.add)
+        tt(dg, ind(sl(um, 64, 192), J8), mJ, AL.add)
         scan(stream(4, 128), rbA, dg, AL.add, AL.min)
         scan(stream(0), sl(rbA, 0, 64), key, AL.add, AL.min)
         scan(stream(1), TH, key, AL.max, AL.min)
@@ -387,23 +434,22 @@ def build(T, rank, core, topo, cfg):
         pf, pl = new(F_, 64), new(U_, 64)
         tt(pf, ind(efw, hbl), cP, AL.add)
         ts(pl, pf, 0.0625, AL.mult, -0.46875, AL.add)
-        pv = cfg["lastv"] if last else cfg["pv"]
-        wide(A2, A, pl, ((0, pv, "v"), (pv, 64, "s")))
-        X = X1
-        iv = cfg["lastv"] if last else cfg["iv"]
-        wide(X, A2, invl, ((0, iv, "v"), (iv, 64, "s")))
+        wide(A2, A, pl, cfg["sites0" if last else "slots"])
+        site[0] = 1900
+        if home:
+            wide(X1, A2, invl, cfg["out" if last else "back"])
         if last:
-            dma("y", lambda: T.y[:, 0:16 * iv], lambda: ap(sl(X1, 0, 16 * iv)), [sl(X1, 0, 16 * iv)], None, 131072)
-            dma("s", lambda: T.y[:, 16 * iv:V], lambda: ap(sl(X1, 16 * iv, V)), [sl(X1, 16 * iv, V)], None, 131072)
+            for a, b, e in cfg["out"]:
+                dma("s" if b == 64 else "y", lambda a=a, b=b: T.y[:, 16 * a:16 * b],
+                    lambda a=a, b=b: ap(sl(X1, 16 * a, 16 * b)), [sl(X1, 16 * a, 16 * b)], None, 4096 * (b - a))
             break
         site[0] = 2000
         kc = ends(0)
-        z, zz, rc, cls, lst = col(), new(F_, 4), col(), col(), new(U_, 4)
-        act(zz, kc, bias=zb, total=z)
-        mm(P("pc", 0, 1), twos, z, True, True)
-        ts(rc, P("pc", 0, 1), 1.5 * 2 ** 32, AL.add, 1.5 * 2 ** 32, AL.subtract)
-        ts(cls, P("pc", 0, 1), rc, AL.subtract)
-        ts(lst, base2, cls, AL.add)
+        cls, lst = new(F_, 15), new(U_, 4)
+        mm(P("pc", 0, 4), twos, kc, True, True)
+        mm(P("pc", 7, 11), twos, kc, True, True)
+        scan(cls, turn, P("pc", 0, 15), AL.mult, AL.add)
+        cp(lst, sl(cls, 11, 15))
         win = nb
         sJ, Sg = new(B_, 64), new(B_, 4)
         gather("s", sJ, Z, JZ)
@@ -414,49 +460,57 @@ def build(T, rank, core, topo, cfg):
             mm(P("pp", d, 4), hB, sl(Sg, 0, 4 - d), False, False)
         for r in range(4):
             mm(P("pp", r, r + 1), Dr[r], sl(Sg, r, r + 1), False, r == 3)
-        mm(P("pc", 0, 1), Id, sl(cPos, 4, 5), True, False)
+        mm(P("pc", 16, 17), Id, sl(cPos, 4, 5), True, False)
         for r in range(4):
-            mm(P("pc", 0, 1), hB, sl(Sg, r, r + 1), False, r == 3)
+            mm(P("pc", 16, 17), hB, sl(Sg, r, r + 1), False, r == 3)
         posl = new(U_, 4)
         cp(posl, P("pp", 0, 4))
-        CW = sl(CWall, 208 * t, 208 * t + 208)
-        cp(ind(sl(CW, 0, 192), posl), sJ)
-        sL, sR = sl(CW, 176, 192), sl(CW, 192, 208)
-        rland = new(I_, 16)
+        cp(ind(CW, posl), sJ)
+        sZ, sL = sl(CW, 16 * 176, 16 * 192), sl(CW, 16 * 176, 16 * 192, 16)
         hop = 1 + t % (N - 1)
-        if t < cfg["early"]:
-            sJR, posR, CR = new(B_, 64), new(U_, 4), sl(CWall, 208 * (STEPS - 1), 208 * (STEPS - 1) + 192)
-            send(sJ, sJR, (rank + hop) % N, "sig")
-            send(posl, posR, (rank + hop) % N, "req%d" % t)
-            cp(ind(CR, posR), sJR)
-            sR = sl(CR, 176, 192)
+        um2, hq, hl2, rland = new(I_, 96), new(U_, 16), new(U_, 16), new(I_, 16)
+        hashes(um2, 32, [(0, W1, W2, sL), (16,) + WR[hop] + (sL,)], C2, "pr", "ps")
+        h0 = sl(um2, 64, 80)
+        cp(hq, sl(um2, 80, 96))
+        sq, SE2 = new(B_, 256), new(B_, 256)
+        if cfg["far"]:
+            scan(sq, sl(keep, 0, 256), sZ, AL.mult, AL.add)
+            send(sq, SE2, (rank + hop) % N, "sig%d" % t, cfg["far"])
         else:
-            send(sL, sR, (rank + hop) % N, "req%d" % t)
+            sR = new(B_, 16)
+            act(sl(sq, 0, 16), sL)
+            send(sl(sq, 0, 16), sR, (rank + hop) % N, "sig%d" % t)
+            if "sq" in ons:
+                gather("s", SE2, sR, rep16)
+            else:
+                act(sl(Z2, 0, 256, 16), sR)
+                scan(SE2, sl(keep, 0, 256), Z2, AL.mult, AL.add)
+        send(hq, hl2, (rank + hop) % N, "req%d" % t)
         site[0] = 3000
-        if cfg["merge"]:
-            um2 = new(I_, 96)
-            terms = [(0, W1, W2, sL), (16, W1, W2, sR)] if t < cfg["early"] else [(0, W1, W2, sl(CW, 176, 208))]
-            hashes(um2, 32, terms, C2, "pr", "ps")
-            h0, hR = sl(um2, 64, 80), sl(um2, 80, 96)
+        if "d2" in ons:
+            mm(P("pr", 0, 256), nId, SE2, True, False)
+            gather("s", D2, tagw, hl2)
+            mm(P("pr", 0, 256), Id, D2, False, True)
+        elif "x2" in ons:
+            gather("s", D2, tagw, hl2)
+            tt(R2, ind(tagw, hl2), SE2, AL.max)
         else:
-            um2, um3 = new(I_, 48), new(I_, 48)
-            hashes(um2, 16, [(0, W1, W2, sL)], C0, "pr", "ps")
-            hashes(um3, 16, [(0, W1, W2, sR)], sl(C2, 16, 48), "pr", "ps")
-            h0, hR = sl(um2, 32, 48), sl(um3, 32, 48)
-        hl2 = new(U_, 16)
-        cp(hl2, hR)
-        if "se2" in ons:
-            gather("s", SE2, sR, rep16)
-        else:
-            cp(sl(Z2, 0, 256, 16), sR)
-            scan(SE2, sl(keep, 0, 256), Z2, AL.mult, AL.add)
-        tt(D2, ind(tagw, hl2), SE2, AL.subtract)
-        gather("s", E2, sl(ef, 0, H), hl2)
+            tt(D2, ind(tagw, hl2), SE2, AL.subtract)
+        gather("s" if "e2" in ons else "v", E2, sl(ef, 0, H), hl2)
         key2 = P("pq", 0, 64)
         mm(key2, Id, K2, True, False)
-        act(R2, D2, AF.Abs)
+        if "r2" in ons:
+            act(R2, P("pr", 0, 256) if "d2" in ons else D2, AF.Abs)
+        else:
+            if "x2" in ons:
+                for a in range(4):
+                    mm(key2, sl(W4n, 12 - 4 * a, 140 - 4 * a), sl(SE2, 64 * a, 64 * a + 64), False, False)
+            else:
+                ts(R2, D2, 0.0, AL.max)
+            for a in range(4):
+                mm(key2, sl(W4n, 12 - 4 * a, 140 - 4 * a), sl(D2, 64 * a, 64 * a + 64), False, False)
         for a in range(4):
-            mm(key2, sl(W4, 12 - 4 * a, 140 - 4 * a), sl(R2, 64 * a, 64 * a + 64), False, a == 3)
+            mm(key2, sl(W4 if "r2" in ons else W4p, 12 - 4 * a, 140 - 4 * a), sl(R2, 64 * a, 64 * a + 64), False, a == 3)
         bm, eq, junk, h0c, cnt, wl = new(F_, 32), new(F_, 17), new(F_, 17), col(), col(), new(U_, 1)
         tt(bm, ind(h0, dup), MK, AL.add)
         if "h0c" in ons:
@@ -464,11 +518,11 @@ def build(T, rank, core, topo, cfg):
         else:
             red(h0c, sl(bm, 16, 32), AL.max)
         if "eq" in ons:
-            act(sl(eq, 16, 17), P("pc", 0, 1), AF.Relu, scale=-1.0)
+            act(sl(eq, 16, 17), P("pc", 16, 17), AF.Relu, scale=-1.0)
             act(sl(eq, 0, 16), sl(bm, 0, 16), AF.Abs, scale=-1.0, bias=h0c)
             act(new(F_, 17), eq, AF.Relu, scale=-4096.0, bias=4096.0, total=cnt)
         else:
-            act(sl(eq, 16, 17), P("pc", 0, 1), AF.Relu, scale=4096.0, bias=4096.0)
+            act(sl(eq, 16, 17), P("pc", 16, 17), AF.Relu, scale=4096.0, bias=4096.0)
             ts(sl(eq, 0, 16), sl(bm, 0, 16), h0c, AL.is_equal, 4096.0, AL.mult)
             red(cnt, eq, AL.max)
         ts(wl, cnt, h0c, AL.max, dum, AL.min)
@@ -512,8 +566,7 @@ def depend(ops, exact):
                 h.append((k, isw, r))
         dep.discard(k)
         o["dep"] = sorted(dep)
-        o["hop"] = [0 if (ops[j]["e"] == "p" and o["e"] == "p") or o["e"] == "x" else (1 if ops[j]["e"] == o["e"] else ACROSS)
-                    for j in o["dep"]]
+        o["hop"] = [0 if o["e"] == "x" else ACROSS if ops[j]["e"] != o["e"] else int(o["e"] != "p") for j in o["dep"]]
 
 
 def times(ops, m):
@@ -521,18 +574,29 @@ def times(ops, m):
     return c, [o["lat"][0] + o["lat"][1] * m[5] + o["lat"][2] * m[6] for o in ops]
 
 
-def replay(ops, order, c, lat, hop):
-    fin, free = [0.0] * len(ops), {}
-    for k in order:
-        o = ops[k]
-        st = free.get(o["e"], 0.0)
-        for j, h in zip(o["dep"], o["hop"]):
-            if fin[j] + h * hop > st:
-                st = fin[j] + h * hop
-        if o["e"] != "x":
-            free[o["e"]] = st + c[k]
-        fin[k] = st + c[k] + lat[k]
-    return fin
+def nodes_of(ops):
+    anc, pd, ns = [], [], [0] * len(ops)
+    for o in ops:
+        m = 0
+        for j in o["dep"]:
+            m |= anc[j]
+        pd.append([(j, h) for j, h in zip(o["dep"], o["hop"]) if not m >> j & 1])
+        for j, h in pd[-1]:
+            m |= 1 << j
+            ns[j] += 1
+        anc.append(m)
+    nodes, of = [], []
+    for k, o in enumerate(ops):
+        if o["e"] == "p" and len(pd[k]) == 1 and ops[pd[k][0][0]]["e"] == "p" and ns[pd[k][0][0]] == 1:
+            z = nodes[of[pd[k][0][0]]]
+            z["ops"].append(k)
+            z["c"] = tuple(a + b for a, b in zip(z["c"], o["c"]))
+            of.append(of[pd[k][0][0]])
+        else:
+            of.append(len(nodes))
+            nodes.append({"ops": [k], "e": o["e"], "c": o["c"], "lat": o["lat"], "site": o["site"],
+                          "dep": [of[j] for j, h in pd[k]], "hop": [h for j, h in pd[k]]})
+    return nodes
 
 
 def schedule(ops, c, lat, hop, bias):
@@ -577,21 +641,46 @@ def schedule(ops, c, lat, hop, bias):
 
 
 def plan(ops, cfg):
+    ops = nodes_of(ops)
+    n = len(ops)
     tm = [times(ops, m) + (m[4],) for m in MODELS]
+    gap = [[[(j, lat[j] + h * hop) for j, h in zip(o["dep"], o["hop"])] for o in ops] for c, lat, hop in tm]
+    ends = [k for k, o in enumerate(ops) if o["lat"][1]][-4:]
+    eng = [o["e"] for o in ops]
     state = [cfg["seed"]]
 
     def rnd():
         state[0] = (state[0] * 6364136223846793005 + 1442695040888963407) % (1 << 64)
         return (state[0] >> 33) / float(1 << 31)
 
-    def score(order):
-        return [max(replay(ops, order, *z)) for z in tm]
-    total = lambda s: s[0] + sum(s)
-    n = len(ops)
-    bias = [0.0] * n
+    def before(order):
+        prev, last = [n] * n, {}
+        for k in order:
+            if eng[k] != "x":
+                prev[k] = last.get(eng[k], n)
+                last[eng[k]] = k
+        return prev
+
+    def replay(part, prev, old):
+        new, s = [], []
+        for (c, lat, hop), g, ex in zip(tm, gap, old):
+            ex = list(ex)
+            for k in part:
+                t = ex[prev[k]]
+                for j, d in g[k]:
+                    d += ex[j]
+                    if d > t:
+                        t = d
+                ex[k] = t + c[k]
+            new.append(ex)
+            s.append(max([ex[k] + lat[k] for k in ends]) + cfg["mean"] * sum(ex) / n)
+        return new, s
+    zero = [[0.0] * (n + 1) for _ in tm]
+    total = lambda s: sum(x * m[7] for x, m in zip(s, MODELS))
+    bias = [cfg["ahead"] * (2000 < o["site"] < 2006 or 1000 < o["site"] < 1050) for o in ops]
     order = schedule(ops, *tm[0], bias)
-    best = score(order)
-    pick = [k for k, o in enumerate(ops) if o["e"] in "vsg"]
+    best = replay(order, before(order), zero)[1]
+    pick = [k for k in range(n) if eng[k] in "vsg"]
     same = {}
     for k, o in enumerate(ops):
         same.setdefault(o["site"], []).append(k)
@@ -602,60 +691,84 @@ def plan(ops, cfg):
             for j in (same[ops[k]["site"]] if rnd() < 0.5 else [k]):
                 b[j] += d
         o = schedule(ops, *tm[0], b)
-        s = score(o)
+        s = replay(o, before(o), zero)[1]
         if total(s) <= total(best):
             bias, order, best = b, o, s
     succ = [[] for _ in range(n)]
     for k, o in enumerate(ops):
         for j in o["dep"]:
             succ[j].append(k)
+    prev, at = before(order), [0] * n
+    ex = replay(order, prev, zero)[0]
     now, top, kept = total(best), total(best), list(order)
     for it in range(cfg["swaps"]):
-        if it % 8 == 0:
-            c, lat, hop = tm[int(rnd() * len(tm))]
-            fin = replay(ops, order, c, lat, hop)
-            at = {k: i for i, k in enumerate(order)}
-            order.sort(key=lambda k: (fin[k] - c[k] - lat[k], at[k]))
-            prev, lastof = {}, {}
-            for k in order:
-                prev[k] = lastof.get(ops[k]["e"])
-                lastof[ops[k]["e"]] = k
-            pairs, k = [], max(range(n), key=lambda z: fin[z])
-            while k is not None:
-                st, j = fin[k] - c[k] - lat[k], prev[k]
-                nxt = None
-                for d, h in zip(ops[k]["dep"], ops[k]["hop"]):
-                    if abs(fin[d] + h * hop - st) < 1e-6:
-                        nxt = d
-                if nxt is None and j is not None and ops[k]["e"] != "x":
-                    pairs.append((j, k))
-                    nxt = j
+        if it % 16 == 0:
+            m = int(rnd() * len(tm))
+            c, x = tm[m][0], ex[m]
+            order.sort(key=lambda k: x[k] - c[k])
+            for i, k in enumerate(order):
+                at[k] = i
+            pairs, k = [], max(ends, key=lambda z: x[z] + tm[m][1][z])
+            while k != n:
+                nxt = n
+                for j, d in gap[m][k]:
+                    if abs(x[j] + d + c[k] - x[k]) < 1e-6:
+                        nxt = j
+                if nxt == n and prev[k] != n:
+                    nxt = prev[k]
+                    pairs.append((nxt, k))
                 k = nxt
-        if rnd() < 0.7 and pairs:
+        side = rnd() < 0.5
+        if rnd() < 0.6 and pairs:
             j, k = pairs[int(rnd() * len(pairs))]
-            while rnd() < 0.4 and prev[j] is not None:
-                j = prev[j]
         else:
-            k = pick[int(rnd() * len(pick))]
-            j = prev[k]
-            if j is None:
+            k = j = pick[int(rnd() * len(pick))]
+        if k == j or rnd() < cfg["long"]:
+            if side:
+                free = [z for z in order[max([at[d] for d in ops[k]["dep"]] + [at[k] - 120, -1]) + 1:at[k]] if eng[z] == eng[k]]
+            else:
+                free = [z for z in order[at[j] + 1:min([at[d] for d in succ[j]] + [at[j] + 120])] if eng[z] == eng[j]]
+            if not free:
                 continue
-        a, b = order.index(j), order.index(k)
-        if a > b:
+            z = int(rnd() * rnd() * len(free))
+            j, k = (free[-1 - z], k) if side else (j, free[z])
+        moves = [(j, k)]
+        if rnd() < cfg["joint"]:
+            sj, sk = same[ops[j]["site"]], same[ops[k]["site"]]
+            d = sj.index(j) - sk.index(k)
+            moves = [(sj[i + d], sk[i]) for i in range(len(sk)) if 0 <= i + d < len(sj)]
+        o, pos, p, low = list(order), list(at), list(prev), n
+        for j, k in moves:
+            a, b = pos[j], pos[k]
+            if a > b:
+                continue
+            early = all(pos[d] < a for d in ops[k]["dep"])
+            late = all(pos[d] > b for d in succ[j])
+            if early and (side or not late):
+                mid = [k] + o[a:b]
+            elif late:
+                mid = o[a + 1:b + 1] + [j]
+            else:
+                continue
+            o[a:b + 1] = mid
+            last = p[j]
+            for i, z in enumerate(mid):
+                pos[z] = a + i
+                if eng[z] == eng[k]:
+                    p[z], last = last, z
+            for z in o[b + 1:]:
+                if eng[z] == eng[k]:
+                    p[z] = last
+                    break
+            low = min(low, a)
+        if low == n:
             continue
-        mid = set(order[a:b + 1])
-        if not any(d in mid for d in ops[k]["dep"]) and (rnd() < 0.5 or any(d in mid for d in succ[j])):
-            o = order[:a] + [k] + order[a:b] + order[b + 1:]
-        elif not any(d in mid for d in succ[j]):
-            o = order[:a] + order[a + 1:b + 1] + [j] + order[b + 1:]
-        else:
-            continue
-        s = score(o)
+        x, s = replay(o[low:], p, ex)
         if total(s) <= now + cfg["heat"] * (1.0 - it / cfg["swaps"]) * rnd() * rnd():
-            order, now = o, total(s)
+            now, prev, ex, order, at = total(s), p, x, o, pos
             if now < top:
-                top, kept, best = now, list(o), s
-    return kept, best
+                top, kept, best = now, list(order), s
+    return [k for z in kept for k in ops[z]["ops"]], best
 
 
 def emit(g, T, ops, order):
@@ -663,9 +776,7 @@ def emit(g, T, ops, order):
     csem = {"v": "cv", "s": "cs", "p": "cp", "g": "cg"}
     need = set()
     for o in ops:
-        for j in o["dep"]:
-            if not (ops[j]["e"] == "p" and o["e"] == "p"):
-                need.add(j)
+        need.update(j for j, h in zip(o["dep"], o["hop"]) if h or o["e"] == "x")
     clock = {e: {} for e in queue}
     count = {}
     mark = {}
@@ -677,7 +788,7 @@ def emit(g, T, ops, order):
             count[o["sem"][0]] = o["sem"][1]
             continue
         q, ck = queue[e], clock[e]
-        want = [mark[j] for j in o["dep"] if j in mark and not (ops[j]["e"] == "p" and e == "p")]
+        want = [mark[j] for j, h in zip(o["dep"], o["hop"]) if j in mark and h]
         for (s, v, c) in sorted(want, key=lambda z: -z[1]):
             if ck.get(s, 0) < v and not any(c2.get(s, 0) >= v and ck.get(s2, 0) < v2 and s2 != s for (s2, v2, c2) in want):
                 q.wait_ge(T.sem[s], v)

from concourse.mybir import AluOpType, AxisListType, ActivationFunctionType

AL = AluOpType
AF = ActivationFunctionType
SCRATCH = {
    "ab": ("sbuf", [128, 28672], "bfloat16"),
    "af": ("sbuf", [128, 8192], "float32"),
    "ai": ("sbuf", [128, 5120], "int32"),
    "au": ("sbuf", [128, 2560], "uint16"),
}
PSUM = ("pu", "pw", "pk", "pp", "pc", "pr", "ps", "pq")
SCRATCH.update({p: ("psum", [128, 512], "float32") for p in PSUM})
STEPS, V, H = 5, 1024, 2048
SEMAPHORES = (["cv", "cs", "cp", "cg", "sent", "wt1", "wt2", "wt3"] + ["d%d" % k for k in range(16)]
              + [s + str(t) for s in ("sig", "req", "rep") for t in range(STEPS - 1)])
SIZE = {"ab": 2, "af": 4, "ai": 4, "au": 2}

CFG = {"sites": ((0, 24, "v"), (24, 46, "s"), (46, 64, "s")), "sites0": ((0, 32, "v"), (32, 64, "s")),
       "slots": ((0, 28, "v"), (28, 64, "s")), "back": ((0, 32, "v"), (32, 64, "s")),
       "out": ((0, 20, "v"), (20, 32, "v"), (32, 52, "s"), (52, 64, "s")), "spread": (512, 512),
       "chunks": ((0, 5, "a"), (5, 5, "a"), (10, 4, "a"), (14, 2, "a")),
       "parts": (12, 12, 12, 12, 8, 8), "on_s": ("s", "r2", "e2", "h0c", "eq"), "first": 2500, "deal": (64,), "home": 0, "far": 0,
       "exact": 1, "iters": 100, "swaps": 140000, "heat": 2500.0, "mean": 0.5, "joint": 0.5, "long": 0.5, "ahead": 0.0, "seed": 1}
MODELS = ((0.85, 1.3, 3.15, 0.65, 200.0, 1800.0, 2300.0, 1.0), (1.0, 1.6, 3.9, 0.8, 200.0, 2000.0, 2600.0, 0.9),
          (1.25, 2.3, 7.0, 0.9, 220.0, 2400.0, 2600.0, 0.6), (1.0, 1.3, 2.5, 0.9, 250.0, 2400.0, 3500.0, 0.8))
ACROSS = 1.0
ORDER = {}


def nel(r):
    return len(range(r[1], r[2], r[3]))


def sl(r, a, b, s=1):
    return (r[0], r[1] + a, r[1] + b, s)


def build(T, rank, core, topo, cfg):
    ops = []
    top = {"ab": 0, "af": 0, "ai": 0, "au": 0}
    ons = cfg["on_s"]
    site = [0]

    def new(a, n):
        q = 32 // SIZE[a]
        s = top[a]
        top[a] = s + (n + q - 1) // q * q
        assert top[a] <= SCRATCH[a][1][1], a
        return (a, s, s + n, 1)

    def ap(r):
        if r[0] == "ind":
            return ap(r[1]).indirect(ap(r[2]))
        if r[3] == 1:
            return T[r[0]][:, r[1]:r[2]]
        return T[r[0]][:, r[1]:r[2]:r[3]]

    def val(x):
        return ap(x) if isinstance(x, tuple) else x

    def add(eng, fn, ins, out, cost, kind="c", lat=(0, 0, 0), after=(), sem=None, out2=None):
        rd, wr = [], []
        for x in ins:
            if isinstance(x, tuple):
                rd += [x[1], x[2]] if x[0] == "ind" else [x]
        if out is not None:
            if out[0] == "ind":
                wr, rd = [out[1]], rd + [out[2]]
            else:
                wr = [out]
        if out2 is not None:
            wr.append(out2)
        site[0] += 1
        ops.append({"site": site[0], "e": eng, "fn": fn, "r": rd, "w": wr, "c": cost, "k": kind, "lat": lat,
                    "after": list(after), "sem": sem})
        return len(ops) - 1

    def ind(win, off):
        return ("ind", win, off)

    def two(xs):
        return all(x[0] in ("ab", "au") for x in xs)

    def size(out, ins, f, fix=0):
        if out[0] == "ind":
            return (50 + fix, 0, 0, 16 * nel(out[2]), 0)
        if ins and ins[0][0] == "ind":
            return (50 + fix, 0, 16 * nel(ins[0][2]), 0, 0)
        return (fix, max(64, f * nel(ins[0] if ins else out)), 0, 0, 0)

    def cp(out, a):
        return add("v", lambda q: q.tensor_copy(ap(out), ap(a)), [a], out, size(out, [a], 0.5 if two([out, a]) else 1))

    def ts(out, a, s1, o0, s2=None, o1=None):
        if o1 is None:
            fn = lambda q: q.tensor_scalar(ap(out), ap(a), val(s1), None, o0)
        else:
            fn = lambda q: q.tensor_scalar(ap(out), ap(a), val(s1), val(s2), o0, o1)
        return add("v", fn, [a, s1, s2], out, size(out, [a], 0.5 if two([out, a]) else 1))

    def tt(out, a, b, o):
        f = 1 if a[0] in PSUM or b[0] in PSUM else 2
        return add("v", lambda q: q.tensor_tensor(ap(out), ap(a), ap(b), o), [a, b], out, size(out, [a], f))

    def scan(out, a, b, o0, o1, first=0.0):
        f = 0.5 if two([out, a, b]) else 1
        return add("v", lambda q: q.tensor_tensor_scan(ap(out), ap(a), ap(b), first, o0, o1), [a, b], out, size(out, [a], f))

    def red(out, a, o):
        return add("v", lambda q: q.tensor_reduce(ap(out), ap(a), AxisListType.X, o), [a], out, size(out, [a], 1))

    def ms(out, c):
        return add("v", lambda q: q.memset(ap(out), c), [], out, size(out, [], 0.5 if two([out]) else 1))

    def act(out, a, func=AF.Identity, bias=None, scale=None, total=None):
        kw = {k: x for k, x in (("bias", bias), ("scale", scale), ("accum_out", total)) if x is not None}
        return add("s", lambda q: q.activation(ap(out), ap(a), func, **{k: val(x) for k, x in kw.items()}),
                   [a, bias, scale], out, size(out, [a], 1, 35 if total else 15), out2=total)

    def mm(out, l, r, start, stop):
        n = max(64, nel(r)) * (4 if l[0] == "af" else 1)
        return add("p", lambda q: q.matmul(ap(out), ap(l), ap(r), start, stop), [l, r], out, (0, 0, 0, 0, n))

    def iota(out, pat, base, cm=0):
        if out[0] == "ai":
            fn = lambda q: q.iota(ap(out), pat, base, cm)
        else:
            fn = lambda q: q.iota(ap(out), pat, base, cm, allow_small_or_imprecise_dtypes=True)
        return add("g", fn, [], out, (130, 2 * nel(out), 0, 0, 0))

    nd, nr = [0], []

    def dma(eng, fo, fi, ins, out, nbytes, after=()):
        s = "d%d" % nd[0]
        nd[0] += 1
        return add(eng, lambda q: q.dma_start(fo(), fi()), ins, out, (60, 0, 0, 0, 0), "d", (nbytes / 200.0, 1, 0), after, s)

    def send(src, land, dst_rank, sem, more=0):
        dst = T.cores[dst_rank]
        rid, pid = topo.addr(dst, core)
        m = topo.mask(core, dst)
        n = len(topo.engines(core, dst))
        k = add("g", lambda q: q.remote_dma(ap(land), ap(src), T.sem[sem], T.sem.sent, pid, rid, m), [src], None,
                (300 + (0 if nr else cfg["first"]), 0, 0, 0, 0), "r", after=nr[:1], sem=n)
        nr.append(k)
        return add("x", None, [], land, (0, 0, 0, 0, 0), "x", (more, 0, 1), [k], (sem, n))

    def gather(e, out, win, lst):
        return cp(out, ind(win, lst)) if e == "v" else act(out, ind(win, lst), AF.Copy)

    def wide(out, win, lst, parts):
        for a, b, e in parts:
            gather(e, sl(out, 16 * a, 16 * b), win, sl(lst, a, b))

    B_, F_, I_, U_ = "ab", "af", "ai", "au"
    N = len(T.cores)
    X0, tag, ef = new(B_, V), new(B_, H + 32), new(B_, H + 32)
    nb0, nb, wb, thi = new(I_, 64), new(I_, 512), new(B_, 2), new(I_, 1)
    c0 = rank % 8
    k0 = dma("y", lambda: ap(nb0), lambda: T.nb[:, 64 * c0:64 * c0 + 64], [], nb0, 32768)
    kx = dma("s", lambda: ap(X0), lambda: T.x[:], [], X0, 262144)
    dma("s", lambda: ap(wb), lambda: T.w[:], [], wb, 262144)
    dma("s", lambda: ap(thi), lambda: T.th[:], [], thi, 262144)
    dma("y", lambda: ap(sl(tag, 0, H)), lambda: T.tag[:], [], sl(tag, 0, H), 786432)
    dma("y", lambda: ap(sl(ef, 0, H)), lambda: T.ef[:], [], sl(ef, 0, H), 786432, [k0])
    dma("y", lambda: ap(nb), lambda: T.nb[:], [], nb, 786432, [kx])

    def col():
        return new(F_, 1)
    BIG = float(1 << 19)
    pI, t1, t2 = new(I_, 1), new(I_, 1), new(I_, 1)
    iota(pI, [[0, 1]], 0, 1)
    io = new(B_, 144)
    iota(io, [[1, 144]], 0)
    Kw = new(B_, 64)
    iota(Kw, [[0, 4], [1, 16]], 0)
    bI = new(B_, 64)
    iota(bI, [[1, 4], [0, 16]], 0)
    vals = new(F_, V)
    iota(sl(vals, 0, 512), [[16, 8], [256, 4], [1, 16]], 32)
    iota(sl(vals, 512, V), [[16, 8], [256, 4], [1, 16]], 160)
    cP = new(F_, 64)
    iota(cP, [[256, 4], [1024, 16]], 0)
    CW = new(B_, 16 * 192)
    iota(sl(CW, 16 * 176, 16 * 192), [[0, 256]], 0)
    if "sq" in ons:
        rep16 = new(U_, 16)
        cp(rep16, sl(io, 0, 16))
    elif not cfg["far"]:
        Z2 = new(B_, 256)
        iota(Z2, [[0, 256]], 0)
    lane, pF, l4, colb, lane4, c15, cb, c4, cl, hl_ = [col() for _ in range(10)]
    ts(t1, pI, 15, AL.bitwise_and)
    cp(lane, t1)
    ts(t2, pI, 3, AL.bitwise_and)
    cp(l4, t2)
    cp(pF, pI)
    ts(colb, l4, 15.75, AL.mult)
    ts(colb, lane, 0.25, AL.mult, colb, AL.add)
    list0, turn = new(U_, 4), new(F_, 15)
    ts(list0, sl(io, 0, 4), 4.0, AL.mult, colb, AL.add)
    ms(turn, 1.0)
    ms(sl(turn, 7, 8), -1.0)
    for a, b, c in ((4, 5, -224.0), (5, 6, 1.5 * 2 ** 32), (6, 7, -1.5 * 2 ** 32), (12, 15, 4.0)):
        ms(("pc", a, b, 1), c)
    cp(("pc", 11, 12, 1), colb)
    KW = max([512] + [16 * (b - a) for a, b, e in cfg["sites"] + cfg["sites0"]])
    keep, reset, Z, rbA, rbB = new(B_, KW), new(B_, KW), new(B_, V), new(B_, 128), new(B_, 64)
    ms(keep, 1.0)
    ms(sl(keep, 0, KW, 16), 0.0)
    ts(reset, keep, -256.0, AL.mult, 256.0, AL.add)
    ms(Z, 0.0)
    act(rbA, sl(reset, 0, 128), scale=BIG / 256)
    act(rbB, sl(keep, 0, 64), scale=2.0 - BIG, bias=BIG)
    ts(c15, lane, -1.0, AL.mult, pF, AL.add)
    ts(c15, c15, 15.0, AL.add)
    act(cb, c15, scale=-1.0, bias=7.5)
    act(c4, c15, scale=-1.0, bias=1.5)
    act(hl_, lane, scale=-0.5, bias=7.5)
    act(cl, c15, scale=-1.0, bias=hl_)
    act(lane4, lane, scale=4.0)
    io128 = sl(io, 0, 128)
    aB, aL, a4, negB, Id, nL, hB = [new(B_, 144 if k == 2 else 128) for k in range(7)]
    act(aB, io128, AF.Abs, bias=cb)
    ts(negB, aB, 8.0, AL.is_lt, -1.0, AL.mult)
    act(hB, negB, scale=8.0)
    act(aL, io128, AF.Abs, bias=cl)
    ts(nL, aL, hl_, AL.is_le, -8.0, AL.mult)
    W1, W2, N1, N2 = [new(B_, 128) for _ in range(4)]
    ts(W1, aB, 8.0, AL.is_lt, sl(wb, 0, 1), AL.mult)
    ts(W2, aB, 8.0, AL.is_lt, sl(wb, 1, 2), AL.mult)
    WR = {}
    for hop in range(1, N):
        wr, WR[hop] = new(B_, 2), (new(B_, 128), new(B_, 128))
        send(wb, wr, (rank - hop) % N, "wt%d" % hop)
        for k in range(2):
            ts(WR[hop][k], aB, 8.0, AL.is_lt, sl(wr, k, k + 1), AL.mult)
    act(N1, W1, scale=-1.0)
    act(N2, W2, scale=-1.0)
    Wd, W4 = new(B_, 144), new(B_, 144)
    ts(Wd, io, c15, AL.is_equal, 32.0, AL.mult)
    if any(m in "rx" for q, n, m in cfg["chunks"]):
        Wp, Wn = new(B_, 144), new(B_, 144)
        act(Wp, Wd, scale=2.0)
        act(Wn, Wd, scale=-1.0)
    act(a4, io, AF.Abs, bias=c4)
    ts(W4, a4, 2.0, AL.is_lt, 64.0, AL.mult)
    if "r2" not in ons:
        W4p, W4n = new(B_, 144), new(B_, 144)
        act(W4p, W4, scale=2.0)
        act(W4n, W4, scale=-1.0)
    ts(Id, io128, pF, AL.is_equal)
    nId = new(B_, 128)
    act(nId, Id, scale=-1.0)
    Dr = []
    for r in range(4):
        cr, d = col(), new(B_, 128)
        act(cr, lane, scale=8.0, bias=16 * (32.5 + 8 * r))
        act(d, Id, scale=cr)
        Dr.append(d)
    of, OFF = col(), new(B_, 128)
    ts(of, lane, 0.0, AL.is_equal, -0.5, AL.mult)
    act(of, of, bias=64.0)
    silu = act(OFF, io128, AF.Silu, scale=0.0, bias=of)
    ops[silu]["c"] = (1300, 128, 0, 0, 0)
    twos, ones, K2 = new(F_, 128), new(B_, 64), new(B_, 64)
    ms(twos, 2.0)
    ms(ones, 1.0)
    ts(K2, bI, l4, AL.not_equal, BIG, AL.mult)
    cPos, nlane = new(B_, 5), col()
    act(nlane, lane, scale=-16.0, bias=16 * 159.0)
    act(sl(cPos, 0, 4), sl(io, 0, 4), scale=-256.0, bias=nlane)
    act(sl(cPos, 4, 5), lane, scale=-16.0, bias=-16 * 17.0)
    J8, JZ, dup = new(U_, 8), new(U_, 4), new(U_, 2)
    ts(sl(J8, 0, 4), sl(io, 64, 68), lane4, AL.add)
    ts(sl(J8, 4, 8), sl(io, 0, 4), lane4, AL.add)
    ts(JZ, sl(io, 0, 4), lane4, AL.add, 16.0, AL.mult)
    ts(dup, sl(io, 0, 2), 0.0, AL.mult, lane, AL.add)
    m0, mJ, MK = new(B_, 64), new(B_, 128), new(B_, 32)
    ts(m0, Kw, lane, AL.not_equal, BIG / 2, AL.mult)
    act(sl(mJ, 0, 64), m0, bias=60.0 * H)
    act(sl(mJ, 64, 128), m0, bias=float(H))
    ts(sl(MK, 0, 16), sl(Kw, 0, 16), lane, AL.is_le, 4096.0, AL.mult)
    act(sl(MK, 16, 32), sl(m0, 0, 16), scale=-1.0)
    c1, dum, thr, nthr, lane17, cidx, zb = [col() for _ in range(7)]
    act(c1, lane, scale=-64.0, bias=992.0)
    C1, C2 = new(B_, 128), new(B_, 64)
    act(sl(C1, 0, 64), sl(io, 0, 64), scale=0.0, bias=c1)
    act(sl(C1, 64, 128), sl(io, 0, 64), scale=0.0)
    act(sl(C2, 0, 16), sl(io, 0, 16), scale=0.0, bias=32.0)
    act(sl(C2, 16, 64), sl(C1, 48, 96))
    act(dum, lane, bias=float(H + 1))
    TH = new(F_, 64)
    ts(thr, thi, 32.0 / BIG, AL.mult)
    ts(TH, sl(rbA, 0, 64), thr, AL.mult)
    act(nthr, thr, scale=-BIG, bias=-16.0)
    act(lane17, lane, scale=17.0)
    ts(cidx, l4, -1.0, AL.mult, lane, AL.add)
    act(cidx, cidx, scale=16.0, bias=63.0)
    act(sl(ef, H, H + 32), sl(io, 0, 32), scale=0.0, bias=lane17)
    act(sl(tag, H, H + 32), sl(io, 0, 32), scale=0.0)
    Y = new(F_, 720)
    stream = lambda i, n=64: sl(Y, 5 + 16 * i, 5 + 16 * i + 5 * n - 4, 5)
    ends = lambda i, o=0: sl(Y, 80 + o + 16 * i, 80 + o + 16 * i + 241, 80)
    for i, c in enumerate((0.0, -0.75, -4.0, 1.0)):
        ms(ends(i, 320), c)
    c30, part = col(), col()
    act(part, lane, scale=0.0625, bias=128.0 - 15.0 / 32)
    act(c30, lane, scale=2.0, bias=-30.0)
    act(ends(3), sl(io, 0, 4), scale=0.0, bias=c30)

    A, MX, MN, SE, D, R, A2, X1 = [new(B_, V) for _ in range(8)]
    D2, R2, E2 = [new(B_, 256) for _ in range(3)]
    WW = (new(F_, V), new(F_, V))
    tagw, efw = sl(tag, 0, H), sl(ef, 0, H + 32)
    P = lambda n, a, b, s=1: (n, a, b, s)

    def hashes(um, n, terms, const, b1, b2):
        for bank in (b1, b2):
            mm(P(bank, 0, 2 * n), negB if bank == b1 else Id, sl(OFF, 0, 2 * n) if bank == b1 else const, True, False)
            for k, (o, wa, wz, rhs) in enumerate(terms):
                mm(P(bank, o, o + nel(rhs)), wa, rhs, False, False)
                mm(P(bank, n + o, n + o + nel(rhs)), wz, rhs, False, k == len(terms) - 1)
        r, pm = new(F_, 2 * n), new(I_, n)
        ts(r, P(b1, 0, 2 * n), 1.5 * 2 ** 34, AL.add, 1.5 * 2 ** 34, AL.subtract)
        if n > 32:
            tt(P(b1, 256, 256 + n), P(b2, 0, n), sl(r, 0, n), AL.subtract)
            tt(sl(um, n, 2 * n), P(b2, n, 2 * n), sl(r, n, 2 * n), AL.subtract)
            tt(pm, P(b1, 256, 256 + n), sl(um, n, 2 * n), AL.mult)
        else:
            tt(sl(um, 0, 2 * n), P(b2, 0, 2 * n), r, AL.subtract)
            tt(pm, sl(um, 0, n), sl(um, n, 2 * n), AL.mult)
        ts(sl(um, 2 * n, 3 * n), pm, 5, AL.logical_shift_right, H - 1, AL.bitwise_and)

    lst, win = list0, nb0
    for t in range(STEPS):
        last = t == STEPS - 1
        site[0] = 1000
        nbl = new(U_, 64)
        cp(nbl, ind(win, lst))
        segs = cfg["sites"] if t else cfg["sites0"]
        home = last or cfg["home"]
        if t and cfg["home"]:
            site[0] = 1050
            wide(A, X1, nbl, segs)
        elif t:
            for a, b, e in cfg["back"]:
                if e == "v":
                    ts(sl(X1, 16 * a, 16 * b), ind(W, sl(nbl, a, b)), 0.0625, AL.mult, part, AL.add)
                else:
                    act(sl(X1, 16 * a, 16 * b), ind(W, sl(nbl, a, b)), scale=0.0625, bias=part)
            site[0] = 1010
            at, a = new(U_, 64), 0
            for n, bank in zip(cfg["deal"], ("pk", "pq")):
                for k in range(16):
                    mm(P(bank, 0, n), sl(Wd, 15 - k, 143 - k), sl(X1, 16 * a + k, 16 * (a + n), 16), k == 0, k == 15)
                ts(sl(at, a, a + n), P(bank, 0, n), 1.0 / 32, AL.mult, -2080.0, AL.add)
                a += n
            site[0] = 1050
            wide(A, A2, at, segs)
        else:
            site[0] = 1050
            wide(A, X0, nbl, segs)
        nbt, site[0] = nbl, 1060
        if home:
            w1, w2, nbt = new(I_, 64), new(I_, 64), new(U_, 64)
            ts(w1, nbl, 1025.0, AL.mult)
            ts(w2, w1, 4, AL.logical_shift_right, 1023, AL.bitwise_and)
            cp(nbt, w2)
        a, W, site[0] = 0, WW[t % 2], 1070
        for n in cfg["parts"]:
            ops[act(ind(W, sl(nbt, a, a + n)), sl(vals, 16 * a, 16 * (a + n)), AF.Silu)]["after"].append(silu)
            a += n
        if home:
            invf, invl = new(F_, 64), new(U_, 64)
            dma("y", lambda o=invf: ap(o), lambda W=W: T[W[0]][0:128:16, W[1]:W[2]], [W], invf, 32768)
            ts(invl, invf, -31.75, AL.add)
        site[0] = 1090
        for a, b, e in segs:
            scan(sl(MX, 16 * a, 16 * b), sl(keep, 0, 16 * (b - a)), sl(A, 16 * a, 16 * b), AL.mult, AL.max)
            scan(sl(MN, 16 * a, 16 * b), sl(reset, 0, 16 * (b - a)), sl(A, 16 * a, 16 * b), AL.add, AL.min)
        um, hl, site[0] = new(I_, 192), new(U_, 64), 1100
        s, mx, mn = sl(Z, 0, V, 16), sl(MX, 15, V, 16), sl(MN, 15, V, 16)
        hashes(um, 64, [(0, W1, W2, mx), (0, N1, N2, mn)], C1, "pu", "pw")
        cp(hl, sl(um, 128, 192))
        if "s" in ons:
            mm(P("pp", 0, 64), Id, mx, True, False)
            mm(P("pp", 0, 64), nId, mn, False, True)
            act(s, P("pp", 0, 64))
        else:
            tt(s, mx, mn, AL.subtract)
        a = 0
        for n in cfg["spread"]:
            scan(sl(SE, a, a + n), sl(keep, 0, n), sl(Z, a, a + n), AL.mult, AL.add)
            a += n
        key, begun = P("pk", 0, 64), []

        def sums(sel, src, q0, n, stop=False):
            for q in range(q0, q0 + n):
                mm(key, sl(sel, 15 - q, 143 - q), sl(src, 64 * q, 64 * q + 64), not begun, stop and q == q0 + n - 1)
                begun.append(q)
        for q0, n, mode in cfg["chunks"]:
            if mode == "x":
                sums(Wn, SE, q0, n)
        for k, (q0, n, mode) in enumerate(cfg["chunks"]):
            a, b = 64 * q0, 64 * (q0 + n)
            lst4 = sl(hl, 4 * q0, 4 * (q0 + n))
            if mode == "p":
                mm(P("ps", 0, b - a), nId, sl(SE, a, b), True, False)
                gather("s", sl(D, a, b), tagw, lst4)
                mm(P("ps", 0, b - a), Id, sl(D, a, b), False, True)
                act(sl(R, a, b), P("ps", 0, b - a), AF.Abs)
            elif mode == "x":
                gather("s", sl(D, a, b), tagw, lst4)
                tt(sl(R, a, b), ind(tagw, lst4), sl(SE, a, b), AL.max)
            else:
                tt(sl(D, a, b), ind(tagw, lst4), sl(SE, a, b), AL.subtract)
            if mode == "a":
                act(sl(R, a, b), sl(D, a, b), AF.Abs)
            if mode == "r":
                ts(sl(R, a, b), sl(D, a, b), 0.0, AL.max)
            if mode in "rx":
                sums(Wn, D, q0, n)
            sums(Wp if mode in "rx" else Wd, R, q0, n, k == len(cfg["chunks"]) - 1)
        dg, vi, wi, hbl = new(F_, 128), new(I_, 20), new(I_, 4), new(U_, 4)
        tt(dg, ind(sl(um, 64, 192), J8), mJ, AL.add)
        scan(stream(4, 128), rbA, dg, AL.add, AL.min)
        scan(stream(0), sl(rbA, 0, 64), key, AL.add, AL.min)
        scan(stream(1), TH, key, AL.max, AL.min)
        scan(stream(2), rbB, key, AL.add, AL.min)
        scan(vi, sl(Y, 400, 720, 16), sl(Y, 80, 400, 16), AL.mult, AL.add)
        ts(wi, sl(vi, 4, 20, 5), 0x7FFC0000 + H - 1, AL.bitwise_and)
        ts(hbl, wi, float(H), AL.min)
        pf, pl = new(F_, 64), new(U_, 64)
        tt(pf, ind(efw, hbl), cP, AL.add)
        ts(pl, pf, 0.0625, AL.mult, -0.46875, AL.add)
        wide(A2, A, pl, cfg["sites0" if last else "slots"])
        site[0] = 1900
        if home:
            wide(X1, A2, invl, cfg["out" if last else "back"])
        if last:
            for a, b, e in cfg["out"]:
                dma("s" if b == 64 else "y", lambda a=a, b=b: T.y[:, 16 * a:16 * b],
                    lambda a=a, b=b: ap(sl(X1, 16 * a, 16 * b)), [sl(X1, 16 * a, 16 * b)], None, 4096 * (b - a))
            break
        site[0] = 2000
        kc = ends(0)
        cls, lst = new(F_, 15), new(U_, 4)
        mm(P("pc", 0, 4), twos, kc, True, True)
        mm(P("pc", 7, 11), twos, kc, True, True)
        scan(cls, turn, P("pc", 0, 15), AL.mult, AL.add)
        cp(lst, sl(cls, 11, 15))
        win = nb
        sJ, Sg = new(B_, 64), new(B_, 4)
        gather("s", sJ, Z, JZ)
        act(Sg, kc, AF.Sign, bias=nthr)
        mm(P("pp", 0, 4), Id, sl(cPos, 0, 4), True, False)
        mm(P("pp", 0, 4), nL, Sg, False, False)
        for d in (1, 2, 3):
            mm(P("pp", d, 4), hB, sl(Sg, 0, 4 - d), False, False)
        for r in range(4):
            mm(P("pp", r, r + 1), Dr[r], sl(Sg, r, r + 1), False, r == 3)
        mm(P("pc", 16, 17), Id, sl(cPos, 4, 5), True, False)
        for r in range(4):
            mm(P("pc", 16, 17), hB, sl(Sg, r, r + 1), False, r == 3)
        posl = new(U_, 4)
        cp(posl, P("pp", 0, 4))
        cp(ind(CW, posl), sJ)
        sZ, sL = sl(CW, 16 * 176, 16 * 192), sl(CW, 16 * 176, 16 * 192, 16)
        hop = 1 + t % (N - 1)
        um2, hq, hl2, rland = new(I_, 96), new(U_, 16), new(U_, 16), new(I_, 16)
        hashes(um2, 32, [(0, W1, W2, sL), (16,) + WR[hop] + (sL,)], C2, "pr", "ps")
        h0 = sl(um2, 64, 80)
        cp(hq, sl(um2, 80, 96))
        sq, SE2 = new(B_, 256), new(B_, 256)
        if cfg["far"]:
            scan(sq, sl(keep, 0, 256), sZ, AL.mult, AL.add)
            send(sq, SE2, (rank + hop) % N, "sig%d" % t, cfg["far"])
        else:
            sR = new(B_, 16)
            act(sl(sq, 0, 16), sL)
            send(sl(sq, 0, 16), sR, (rank + hop) % N, "sig%d" % t)
            if "sq" in ons:
                gather("s", SE2, sR, rep16)
            else:
                act(sl(Z2, 0, 256, 16), sR)
                scan(SE2, sl(keep, 0, 256), Z2, AL.mult, AL.add)
        send(hq, hl2, (rank + hop) % N, "req%d" % t)
        site[0] = 3000
        if "d2" in ons:
            mm(P("pr", 0, 256), nId, SE2, True, False)
            gather("s", D2, tagw, hl2)
            mm(P("pr", 0, 256), Id, D2, False, True)
        elif "x2" in ons:
            gather("s", D2, tagw, hl2)
            tt(R2, ind(tagw, hl2), SE2, AL.max)
        else:
            tt(D2, ind(tagw, hl2), SE2, AL.subtract)
        gather("s" if "e2" in ons else "v", E2, sl(ef, 0, H), hl2)
        key2 = P("pq", 0, 64)
        mm(key2, Id, K2, True, False)
        if "r2" in ons:
            act(R2, P("pr", 0, 256) if "d2" in ons else D2, AF.Abs)
        else:
            if "x2" in ons:
                for a in range(4):
                    mm(key2, sl(W4n, 12 - 4 * a, 140 - 4 * a), sl(SE2, 64 * a, 64 * a + 64), False, False)
            else:
                ts(R2, D2, 0.0, AL.max)
            for a in range(4):
                mm(key2, sl(W4n, 12 - 4 * a, 140 - 4 * a), sl(D2, 64 * a, 64 * a + 64), False, False)
        for a in range(4):
            mm(key2, sl(W4 if "r2" in ons else W4p, 12 - 4 * a, 140 - 4 * a), sl(R2, 64 * a, 64 * a + 64), False, a == 3)
        bm, eq, junk, h0c, cnt, wl = new(F_, 32), new(F_, 17), new(F_, 17), col(), col(), new(U_, 1)
        tt(bm, ind(h0, dup), MK, AL.add)
        if "h0c" in ons:
            act(sl(junk, 0, 16), sl(bm, 16, 32), AF.Relu, total=h0c)
        else:
            red(h0c, sl(bm, 16, 32), AL.max)
        if "eq" in ons:
            act(sl(eq, 16, 17), P("pc", 16, 17), AF.Relu, scale=-1.0)
            act(sl(eq, 0, 16), sl(bm, 0, 16), AF.Abs, scale=-1.0, bias=h0c)
            act(new(F_, 17), eq, AF.Relu, scale=-4096.0, bias=4096.0, total=cnt)
        else:
            act(sl(eq, 16, 17), P("pc", 16, 17), AF.Relu, scale=4096.0, bias=4096.0)
            ts(sl(eq, 0, 16), sl(bm, 0, 16), h0c, AL.is_equal, 4096.0, AL.mult)
            red(cnt, eq, AL.max)
        ts(wl, cnt, h0c, AL.max, dum, AL.min)
        cp(ind(tag, wl), sL)
        kb, k2, idx, e1, e2 = new(F_, 64), col(), new(U_, 1), new(I_, 16), new(I_, 16)
        scan(kb, ones, key2, AL.add, AL.min, BIG)
        red(k2, key2, AL.min)
        ts(idx, k2, sl(kb, 63, 64), AL.subtract, cidx, AL.add)
        ts(e1, ind(E2, idx), 257.0, AL.mult)
        ts(e2, e1, 4, AL.logical_shift_right, 255, AL.bitwise_and)
        send(e2, rland, (rank - hop) % N, "rep%d" % t)
        cp(ind(ef, wl), rland)
    return ops


def meet(r, z, exact):
    if r[2] <= z[1] or z[2] <= r[1]:
        return False
    if not exact or (r[3] == 1 and z[3] == 1):
        return True
    return not set(range(r[1], r[2], r[3])).isdisjoint(range(z[1], z[2], z[3]))


def depend(ops, exact):
    hist = {}
    for k, o in enumerate(ops):
        dep = set(o["after"])
        for isw, rs in ((False, o["r"]), (True, o["w"])):
            for r in rs:
                for (j, w, z) in hist.get(r[0], []):
                    if r[0] in PSUM:
                        if ops[j]["e"] != o["e"] or w or isw:
                            dep.add(j)
                    elif (w or isw) and meet(r, z, exact):
                        dep.add(j)
        for isw, rs in ((False, o["r"]), (True, o["w"])):
            for r in rs:
                h = hist.setdefault(r[0], [])
                if isw:
                    h[:] = [x for x in h if not (x[2] == r or (r[3] == 1 and r[1] <= x[2][1] and x[2][2] <= r[2]))]
                h.append((k, isw, r))
        dep.discard(k)
        o["dep"] = sorted(dep)
        o["hop"] = [0 if o["e"] == "x" else ACROSS if ops[j]["e"] != o["e"] else int(o["e"] != "p") for j in o["dep"]]


def times(ops, m):
    c = [o["c"][0] + sum(o["c"][i + 1] * m[i] for i in range(4)) for o in ops]
    return c, [o["lat"][0] + o["lat"][1] * m[5] + o["lat"][2] * m[6] for o in ops]


def nodes_of(ops):
    anc, pd, ns = [], [], [0] * len(ops)
    for o in ops:
        m = 0
        for j in o["dep"]:
            m |= anc[j]
        pd.append([(j, h) for j, h in zip(o["dep"], o["hop"]) if not m >> j & 1])
        for j, h in pd[-1]:
            m |= 1 << j
            ns[j] += 1
        anc.append(m)
    nodes, of = [], []
    for k, o in enumerate(ops):
        if o["e"] == "p" and len(pd[k]) == 1 and ops[pd[k][0][0]]["e"] == "p" and ns[pd[k][0][0]] == 1:
            z = nodes[of[pd[k][0][0]]]
            z["ops"].append(k)
            z["c"] = tuple(a + b for a, b in zip(z["c"], o["c"]))
            of.append(of[pd[k][0][0]])
        else:
            of.append(len(nodes))
            nodes.append({"ops": [k], "e": o["e"], "c": o["c"], "lat": o["lat"], "site": o["site"],
                          "dep": [of[j] for j, h in pd[k]], "hop": [h for j, h in pd[k]]})
    return nodes


def schedule(ops, c, lat, hop, bias):
    n = len(ops)
    succ = [[] for _ in range(n)]
    for k, o in enumerate(ops):
        for j, h in zip(o["dep"], o["hop"]):
            succ[j].append((k, h * hop))
    prio = [0.0] * n
    for k in range(n - 1, -1, -1):
        prio[k] = c[k] + lat[k] + max([g + prio[s] for s, g in succ[k]] + [0.0])
    prio = [p + b for p, b in zip(prio, bias)]
    left = [len(o["dep"]) for o in ops]
    rdy = [0.0] * n
    free = {e: 0.0 for e in "vspgyx"}
    cand = {e: [k for k in range(n) if left[k] == 0 and ops[k]["e"] == e] for e in free}
    order = []
    while len(order) < n:
        t0, e = min((max(free[e], min(rdy[k] for k in l)), e) for e, l in cand.items() if l)
        mine = cand[e]
        j = max((prio[k], -k) for k in mine if rdy[k] <= t0)
        j = -j[1]
        best = None
        for h in mine:
            if prio[h] > prio[j] and rdy[h] < t0 + c[j] and (best is None or prio[h] > prio[best]):
                if max(rdy[h] + prio[h], rdy[h] + c[h] + prio[j]) < max(t0 + prio[j], t0 + c[j] + prio[h]):
                    best = h
        if best is not None:
            j = best
        st = max(rdy[j], free[e])
        if e != "x":
            free[e] = st + c[j]
        fin = st + c[j] + lat[j]
        mine.remove(j)
        order.append(j)
        for s, g in succ[j]:
            rdy[s] = max(rdy[s], fin + g)
            left[s] -= 1
            if left[s] == 0:
                cand[ops[s]["e"]].append(s)
    return order


def plan(ops, cfg):
    ops = nodes_of(ops)
    n = len(ops)
    tm = [times(ops, m) + (m[4],) for m in MODELS]
    gap = [[[(j, lat[j] + h * hop) for j, h in zip(o["dep"], o["hop"])] for o in ops] for c, lat, hop in tm]
    ends = [k for k, o in enumerate(ops) if o["lat"][1]][-4:]
    eng = [o["e"] for o in ops]
    state = [cfg["seed"]]

    def rnd():
        state[0] = (state[0] * 6364136223846793005 + 1442695040888963407) % (1 << 64)
        return (state[0] >> 33) / float(1 << 31)

    def before(order):
        prev, last = [n] * n, {}
        for k in order:
            if eng[k] != "x":
                prev[k] = last.get(eng[k], n)
                last[eng[k]] = k
        return prev

    def replay(part, prev, old):
        new, s = [], []
        for (c, lat, hop), g, ex in zip(tm, gap, old):
            ex = list(ex)
            for k in part:
                t = ex[prev[k]]
                for j, d in g[k]:
                    d += ex[j]
                    if d > t:
                        t = d
                ex[k] = t + c[k]
            new.append(ex)
            s.append(max([ex[k] + lat[k] for k in ends]) + cfg["mean"] * sum(ex) / n)
        return new, s
    zero = [[0.0] * (n + 1) for _ in tm]
    total = lambda s: sum(x * m[7] for x, m in zip(s, MODELS))
    bias = [cfg["ahead"] * (2000 < o["site"] < 2006 or 1000 < o["site"] < 1050) for o in ops]
    order = schedule(ops, *tm[0], bias)
    best = replay(order, before(order), zero)[1]
    pick = [k for k in range(n) if eng[k] in "vsg"]
    same = {}
    for k, o in enumerate(ops):
        same.setdefault(o["site"], []).append(k)
    for _ in range(cfg["iters"]):
        b = list(bias)
        for _ in range(1 + int(4 * rnd())):
            k, d = pick[int(rnd() * len(pick))], (rnd() - 0.5) * (4000.0 if rnd() < 0.3 else 800.0)
            for j in (same[ops[k]["site"]] if rnd() < 0.5 else [k]):
                b[j] += d
        o = schedule(ops, *tm[0], b)
        s = replay(o, before(o), zero)[1]
        if total(s) <= total(best):
            bias, order, best = b, o, s
    succ = [[] for _ in range(n)]
    for k, o in enumerate(ops):
        for j in o["dep"]:
            succ[j].append(k)
    prev, at = before(order), [0] * n
    ex = replay(order, prev, zero)[0]
    now, top, kept = total(best), total(best), list(order)
    for it in range(cfg["swaps"]):
        if it % 16 == 0:
            m = int(rnd() * len(tm))
            c, x = tm[m][0], ex[m]
            order.sort(key=lambda k: x[k] - c[k])
            for i, k in enumerate(order):
                at[k] = i
            pairs, k = [], max(ends, key=lambda z: x[z] + tm[m][1][z])
            while k != n:
                nxt = n
                for j, d in gap[m][k]:
                    if abs(x[j] + d + c[k] - x[k]) < 1e-6:
                        nxt = j
                if nxt == n and prev[k] != n:
                    nxt = prev[k]
                    pairs.append((nxt, k))
                k = nxt
        side = rnd() < 0.5
        if rnd() < 0.6 and pairs:
            j, k = pairs[int(rnd() * len(pairs))]
        else:
            k = j = pick[int(rnd() * len(pick))]
        if k == j or rnd() < cfg["long"]:
            if side:
                free = [z for z in order[max([at[d] for d in ops[k]["dep"]] + [at[k] - 120, -1]) + 1:at[k]] if eng[z] == eng[k]]
            else:
                free = [z for z in order[at[j] + 1:min([at[d] for d in succ[j]] + [at[j] + 120])] if eng[z] == eng[j]]
            if not free:
                continue
            z = int(rnd() * rnd() * len(free))
            j, k = (free[-1 - z], k) if side else (j, free[z])
        moves = [(j, k)]
        if rnd() < cfg["joint"]:
            sj, sk = same[ops[j]["site"]], same[ops[k]["site"]]
            d = sj.index(j) - sk.index(k)
            moves = [(sj[i + d], sk[i]) for i in range(len(sk)) if 0 <= i + d < len(sj)]
        o, pos, p, low = list(order), list(at), list(prev), n
        for j, k in moves:
            a, b = pos[j], pos[k]
            if a > b:
                continue
            early = all(pos[d] < a for d in ops[k]["dep"])
            late = all(pos[d] > b for d in succ[j])
            if early and (side or not late):
                mid = [k] + o[a:b]
            elif late:
                mid = o[a + 1:b + 1] + [j]
            else:
                continue
            o[a:b + 1] = mid
            last = p[j]
            for i, z in enumerate(mid):
                pos[z] = a + i
                if eng[z] == eng[k]:
                    p[z], last = last, z
            for z in o[b + 1:]:
                if eng[z] == eng[k]:
                    p[z] = last
                    break
            low = min(low, a)
        if low == n:
            continue
        x, s = replay(o[low:], p, ex)
        if total(s) <= now + cfg["heat"] * (1.0 - it / cfg["swaps"]) * rnd() * rnd():
            now, prev, ex, order, at = total(s), p, x, o, pos
            if now < top:
                top, kept, best = now, list(order), s
    return [k for z in kept for k in ops[z]["ops"]], best


def emit(g, T, ops, order):
    queue = {"v": g.vector, "s": g.scalar, "p": g.tensor, "g": g, "y": g.sync}
    csem = {"v": "cv", "s": "cs", "p": "cp", "g": "cg"}
    need = set()
    for o in ops:
        need.update(j for j, h in zip(o["dep"], o["hop"]) if h or o["e"] == "x")
    clock = {e: {} for e in queue}
    count = {}
    mark = {}
    for k in order:
        o = ops[k]
        e = o["e"]
        if e == "x":
            mark[k] = (o["sem"][0], o["sem"][1], {})
            count[o["sem"][0]] = o["sem"][1]
            continue
        q, ck = queue[e], clock[e]
        want = [mark[j] for j, h in zip(o["dep"], o["hop"]) if j in mark and h]
        for (s, v, c) in sorted(want, key=lambda z: -z[1]):
            if ck.get(s, 0) < v and not any(c2.get(s, 0) >= v and ck.get(s2, 0) < v2 and s2 != s for (s2, v2, c2) in want):
                q.wait_ge(T.sem[s], v)
                ck[s] = v
        for (s, v, c) in want:
            for s2, v2 in c.items():
                if ck.get(s2, 0) < v2:
                    ck[s2] = v2
        ins = o["fn"](q)
        if o["k"] == "r":
            count["sent"] = count.get("sent", 0) + o["sem"]
        elif o["k"] == "d":
            ins.then_inc(T.sem[o["sem"]], 16)
            count[o["sem"]] = 16
            mark[k] = (o["sem"], 16, dict(ck))
        elif k in need:
            s = csem[e]
            count[s] = count.get(s, 0) + 1
            ins.then_inc(T.sem[s], 1)
            mark[k] = (s, count[s], dict(ck))
    for s, v in count.items():
        g.wait_ge(T.sem[s], v)


def rank_program(g, core, T, topo):
    rank = T.rank_of(core)
    if rank is None:
        return
    ops = build(T, rank, core, topo, CFG)
    depend(ops, CFG["exact"])
    if "order" not in ORDER:
        ORDER["order"], ORDER["best"] = plan(ops, CFG)
    emit(g, T, ops, ORDER["order"])
